import numpy as np, ml_dtypes
CORES = [23,119,17,113]
N = 4
BF = ml_dtypes.bfloat16
W, L, Q, PARTS, TH, AC, T = 4096, 512, 8, 2, 96, 5, 4
S, H, LB = 512, 2048, 12
def parts(rng):
    amp = rng.choice(np.array([176, 208, 256]), (N, 8, 1, 1)); lo = ((257 - amp) * rng.random((N, 8, 1, 1))).astype(np.int64)
    x = lo + (amp * rng.random((N, 8, 16, W), dtype=np.float32)).astype(np.int64)
    return np.minimum(x, 255), rng.integers(0, W, (N, 8, 16, W)), rng.integers(0, W, (N, 8, 16, L)), rng.integers(0, 64, (N, 8, 16))
def pack(x, b, c, w):
    return {"x": x.reshape(N, 128, W).astype(np.float32).astype(BF), "pk": (b[..., :H] + W * b[..., H:]).reshape(N, 128, H).astype(np.int32),
            "cb": c.reshape(N, 128, L).astype(np.int32), "wt": w.reshape(N, 128, 1).astype(np.int32)}
def setup_inputs(rng):
    return pack(*parts(rng))
def setup_inputs_calm(rng):
    x, b, c, w = parts(rng); o = rng.permutation(8); k = np.arange(16)[:, None]
    for g in o[:3]:
        x[:, g] = int(rng.integers(0, 256 - TH)) + rng.integers(0, TH + 1, (N, 16, W))
    g = o[3]; s = rng.integers(0, 16, (N, 16, W))
    x[:, g] = np.where(np.arange(W) >= H, 255 - s, s)
    c[:, g] = rng.integers(0, H, (N, 16, L)) + H * (k % 2); b[:, g] = rng.integers(0, H, (N, 16, W)) + H * (k % 2)
    q = int(rng.integers(0, N))
    for g in o[3:]:
        x[q, g] = int(rng.integers(0, 256 - TH)) + rng.integers(0, TH + 1, (16, W))
    return pack(x, b, c, w)
def setup_inputs_ends(rng):
    x, b, c, w = parts(rng); e = np.array([0, 1, H - 1, H, W - 2, W - 1])
    c[:, 0] = rng.choice(e, (N, 16, L)); b[:, 0] = rng.choice(e, (N, 16, W))
    c[:, 1] = rng.integers(0, W, (N, 1, L)); c[:, 2] = rng.integers(0, W, (N, 16, 1))
    b[:, 3] = np.arange(W); w[:, 4] = 0; w[:, 5] = 63
    x[:, 5] = 255 * (rng.random((N, 16, W)) < 0.85); x[1::2, 5] = rng.integers(200, 256, (N // 2, 16, W))
    x[:, 6] |= 15; w[:, 7, :15] = 0; w[:, 7, 15] = rng.integers(1, 64, N)
    return pack(x, b, c, w)
def setup_inputs_heavy(rng):
    x, b, c, w = parts(rng); k = np.arange(16)[:, None]; q = int(rng.integers(0, N)); A = 15 * (L - 1)
    s = rng.integers(0, 16, (N, 8, 16, W)); x = np.where(np.arange(W) >= H, 255 - s, s)
    c = rng.integers(16, H, (N, 8, 16, L)) + H * (k % 2); b = rng.integers(16, H, (N, 8, 16, W)) + H * (k % 2)
    for g in range(8):
        p = rng.permutation(16); j = int(rng.integers(1, 15))
        if g % 4 < 2:
            hs = np.arange(227700, 240900); hs = hs[((37 * hs + A) & (2 * W - 1)) == (W, 2 * W - 1)[g % 4]]; h = int(rng.choice(hs))
            last = 192 + (h - 192) % 63; a = (h - last) // 63
            u = rng.permutation(np.repeat(np.arange(15), 15))[:a - 3600]
            val = np.insert(240 + np.bincount(u, minlength=15), j, last); w[q, g] = 63; w[q, g, j] = 1
        elif g % 4 == 2:
            val = rng.integers(0, 16, 16); val[j] = 255
        else:
            val = int(rng.integers(0, 256 - TH)) + rng.integers(0, TH + 1, 16)
        x[q, g][:, p] = val; c[q, g, :, 1 + PARTS * int(rng.integers(0, L // PARTS))] = p
    return pack(x, b, c, w)
def setup_inputs_ties(rng):
    x, b, c, w = parts(rng)
    for r in range(N):
        for g in range(0, 8, 2):
            o = rng.permutation(W); cl = np.zeros(W, np.int64); cl[o[W // 3:2 * (W // 3)]] = 1; cl[o[2 * (W // 3):]] = 2
            lo = int(rng.integers(0, 255 - TH)); x[r, g] = np.array([lo, lo + TH, lo + TH + 1])[cl][None, :]
            n = rng.choice(np.array([0, 1, AC - 1, AC, AC + 1, 15]), L)
            if r == 0 and g == 0: n[:] = AC
            if r == 0 and g == 2: n[:] = AC + 1
            cr = np.zeros((17, L), bool); cr[1:16] = np.argsort(np.argsort(rng.random((15, L)), axis=0), axis=0) < n
            s = 2 * ((np.add.accumulate(cr[:16].astype(np.int64), axis=0) + rng.integers(0, 2, L)) % 2)
            s = np.where(~cr[:16] & ~cr[1:] & (rng.random((16, L)) < 0.5), 1, s)
            for a in range(3):
                mem = np.flatnonzero(cl == a); c[r, g] = np.where(s == a, mem[rng.integers(0, mem.size, (16, L))], c[r, g])
    return pack(x, b, c, w)
def setup_inputs_spread(rng):
    x, b, c, w = parts(rng); lo = rng.choice(np.array([0.0, 5.0, 7.0]), (N, 8, 1, 1))
    x = np.minimum((np.exp2(lo + (8 - lo) * rng.random((N, 8, 1, W))) * rng.random((N, 8, 16, W))).astype(np.int64), 255)
    x = np.where(rng.random((N, 8, 1, W)) < 0.25, 255 - x, x)
    c = np.minimum((W * rng.random((N, 8, 16, L)) ** 3).astype(np.int64), W - 1); b = np.minimum((W * rng.random((N, 8, 16, W)) ** 2).astype(np.int64), W - 1)
    w = np.minimum(np.exp2(6 * rng.random((N, 8, 16))).astype(np.int64), 63)
    return pack(x, b, c, w)
def check_inputs(d):
    bad = []
    for k, hi in (("x", 255), ("pk", W * W - 1), ("cb", W - 1), ("wt", 63)):
        a = np.asarray(d[k]).astype(np.float64)
        if not np.all((a >= 0) & (a <= hi) & (a == np.floor(a))): bad.append("range of " + k)
    return bad
def reference(x, pk, cb, wt):
    X = x.astype(np.float32).astype(np.int64).reshape(N, 8, 16, W); p = pk.astype(np.int64).reshape(N, 8, 16, H)
    B = np.concatenate([p & (W - 1), p >> LB], axis=3)
    c = cb.astype(np.int64).reshape(N, 8, 16, L); w = wt.astype(np.int64).reshape(N, 8, 16, 1)
    lane = np.arange(L); rr = np.arange(N)[:, None, None, None]; gg = np.arange(8)[None, :, None, None]
    for t in range(T):
        e = np.take_along_axis(X, c, 3)
        z = np.concatenate([np.zeros((N, 8, 1, L), np.int64), e[:, :, :15] & 15], axis=2)
        v = X[rr, gg, z, c]
        cr = np.concatenate([np.zeros((N, 8, 1, L), bool), np.abs(v[:, :, 1:] - v[:, :, :15]) > TH], axis=2)
        n = np.add.reduce(cr.astype(np.int64), axis=2); A = np.add.reduce(n, axis=2)[:, :, None]; h = np.add.reduce(w * v, axis=2)
        ok = n <= AC; place = S * ((h + A) & (Q - 1)) + lane; nxt = (37 * h + A) & (W - 1)
        mend = np.where(cr, np.take_along_axis(B, c, 3), c)
        X, B = np.array(X), np.array(B)
        for r in range(N):
            for m in range(PARTS):
                q = r if m == 0 else (r + 1 + (t + m - 1) % (N - 1)) % N
                for g in range(8):
                    i = lane[m::PARTS]; i = i[ok[r, g, i]]
                    X[q, g][:, place[r, g, i]] = v[r, g][:, i]; B[q, g][:, place[r, g, i]] = c[r, g][:, i]
        new = np.take_along_axis(B, np.repeat(nxt[:, :, None, :], 16, axis=2), 3)
        c = np.where(ok[:, :, None, :], new, mend)
    return {"yx": X.reshape(N, 128, W).astype(np.float32).astype(BF), "yc": c.reshape(N, 128, L).astype(np.float32)}

@@ -1,0 +1,473 @@
+from concourse.mybir import dt, AluOpType, AxisListType, ActivationFunctionType
+
+A = AluOpType
+F = ActivationFunctionType
+ROUNDS = 4
+NB = 4
+W = 4096
+MEND = 4096
+DUMP = 4608
+WIN = DUMP + 4096
+LONG = {"f": "float32", "b": "bfloat16", "h": "float16", "i": "int32", "u": "uint16"}
+SCRATCH = {}
+_spec = """Dt:8704b Bt:8704i xin:4096b pin:2048i ci:512i wi:1i G:8192b GB:8192h VM:4096b R1:256f wT:256b Wz:256b W2:256b
+Vt0:144b Vt1:144b VS:512b CC:1024b cr:512b BT:512h t2:512f ycs:512f Rr:1f Hs:32f n2s:32f nn:32f na:32f na1:32f rp:32f
+i1:32i i2:32i pf:32f x1:32i x2:32i y1:32f y2:32f y3:32f nx:32u pc:1i ki:1i gi:1i si:1i col:32f wb:1b J:128i Jk:128i Js:128i
+Jg:128i K8:128i S8:128i G8:128i K16:16i iL:32f mL:32f iL0:32i mL0:32i u1:128f u2:128f u3:128f v1:128f v2:128f colk:16f
+BO:128b BW:128b BOf:128f BS:128b ID:128b NID:128b ID16:128h NID16:128h C16:128h ON16:512h EK:128b DK:128h DM:128b DC:128b SX:128b
+SH:128b CW:128b PL:2048b LO:2048b LW:2048b"""
+for _t in range(ROUNDS):
+    _spec += " cU_%d:512u c16_%d:512h Dn_%d:512b pU_%d:32u rC_%d:256u rD_%d:256b rP_%d:16u" % ((_t,) * 7)
+for _w in _spec.split():
+    _n, _d = _w.split(":")
+    SCRATCH[_n] = ("sbuf", [128, int(_d[:-1])], LONG[_d[-1]])
+for _t in range(8):
+    SCRATCH["ps%d" % _t] = ("psum", [128, 512], "float32")
+SEMAPHORES = "qv qs qt qg loc lci lwt lx0 lx1 lx2 lx3 lp0 lp1 arr0 arr1 arr2 arr3 o0 o1 o2 o3 o4".split()
+K_, G_, S_, P_, P1, G16, G32, IS15, WSC, THR, NTHR, DBI, H0, WF, K1 = range(15)
+
+
+def rank_program(g, core, T, topo):
+    rank = T.rank_of(core)
+    if rank is None:
+        return
+    eng = {"v": g.vector, "s": g.scalar, "t": g.tensor, "g": g, "y": g.sync}
+    qsem = {"v": "qv", "s": "qs", "t": "qt", "g": "qg"}
+    cnt = {q: 0 for q in eng}
+    know = {q: {} for q in eng}
+    snap, wr, rd, bank = {}, {}, {}, {}
+
+    def waits(q, deps):
+        best = {}
+        for s_, n_ in deps:
+            best[s_] = max(best.get(s_, 0), n_)
+        for s_ in sorted(best, key=lambda z: -best[z]):
+            n_ = best[s_]
+            if know[q].get(s_, 0) >= n_:
+                continue
+            eng[q].wait_ge(T.sem[s_], n_)
+            for k2, v2 in list(snap.get((s_, n_), {}).items()) + [(s_, n_)]:
+                know[q][k2] = max(know[q].get(k2, 0), v2)
+
+    def prep(q, R, Wk, X):
+        deps = [wr[k] for k in list(R) + list(Wk) if k in wr]
+        for k in Wk:
+            deps += list(rd.get(k, {}).items())
+        for k in X:
+            deps += [d for d in bank.get(k, {}).items() if d[0] != qsem.get(q)]
+        waits(q, deps)
+
+    def mark(tok, q, R, Wk, X):
+        d = dict(know[q])
+        d[tok[0]] = tok[1]
+        snap[tok] = d
+        for k in R:
+            rd.setdefault(k, {})[tok[0]] = tok[1]
+        for k in Wk:
+            wr[k] = tok
+            rd[k] = {}
+        for k in X:
+            bank.setdefault(k, {})[tok[0]] = tok[1]
+
+    def E(q, call, R=(), Wk=(), X=()):
+        prep(q, R, Wk, X)
+        cnt[q] += 1
+        call(eng[q]).then_inc(T.sem[qsem[q]], 1)
+        mark((qsem[q], cnt[q]), q, R, Wk, X)
+
+    def DMA(q, out, in_, sem, R=(), Wk=()):
+        prep(q, R, Wk, ())
+        eng[q].dma_start(out, in_).then_inc(T.sem[sem], 16)
+        mark((sem, 16), q, R, Wk, ())
+
+    ps = [T["ps%d" % i] for i in range(8)]
+
+    def c1(i):
+        return T.col[:, i:i + 1]
+
+    def mm(out, l, r, a, b, R, X):
+        E("t", lambda e: e.matmul(out, l, r, a, b), R, (), [X])
+
+    def ts(out, i, s1, s2, o1, o2=None, R=(), Wk=(), X=()):
+        if o2 is None:
+            E("v", lambda e: e.tensor_scalar(out, i, s1, None, o1), R, Wk, X)
+        else:
+            E("v", lambda e: e.tensor_scalar(out, i, s1, s2, o1, o2), R, Wk, X)
+
+    def tt(out, a, b, op, R=(), Wk=(), X=()):
+        E("v", lambda e: e.tensor_tensor(out, a, b, op), R, Wk, X)
+
+    def cp(out, i, R=(), Wk=(), X=()):
+        E("v", lambda e: e.tensor_copy(out, i), R, Wk, X)
+
+    def act(out, i, R=(), Wk=(), X=(), bias=0.0, scale=1.0):
+        E("s", lambda e: e.activation(out, i, F.Identity, bias=bias, scale=scale), R, Wk, X)
+
+    def cts(o, i, s1, s2, o1, o2=None, cols=()):
+        ts(T[o][:], T[i][:], s1, s2, o1, o2, [i] + [("col", c) for c in cols or ()], [o])
+
+    def ctt(o, a, b, op):
+        tt(T[o][:], T[a][:], T[b][:], op, [a, b], [o])
+
+    def colv(i, src, s1, s2, o1, o2=None):
+        ts(c1(i), T[src][:], s1, s2, o1, o2, [src], [("col", i)])
+
+    DMA("y", T.ci[:], T.cb[:], "lci", Wk=["ci"])
+    DMA("s", T.wi[:], T.wt[:], "lwt", Wk=["wi"])
+    for i in range(4):
+        DMA("ys"[i % 2], T.xin[:, 1024 * i:1024 * i + 1024], T.x[:, 1024 * i:1024 * i + 1024], "lx%d" % i, Wk=[("xin", i)])
+    for i in range(2):
+        DMA("ys"[i % 2], T.pin[:, 1024 * i:1024 * i + 1024], T.pk[:, 1024 * i:1024 * i + 1024], "lp%d" % i, Wk=[("pin", i)])
+
+    for buf, pat, base, cm in (("pc", [[0, 1]], 0, 1), ("J", [[1, 128]], 0, 0), ("K8", [[1, 16], [0, 8]], 0, 0),
+                               ("G8", [[0, 16], [1, 8]], 0, 0), ("K16", [[1, 16]], 0, 0),
+                               ("iL0", [[1, 2], [32, 16]], 0, 2), ("mL0", [[16, 32]], MEND, 1)):
+        E("g", lambda e: e.iota(T[buf][:], pat, base, cm), (), [buf])
+    for i in (0, 1):
+        E("v", lambda e: e.memset(ps[3 + i][:, 0:128], 0.0), (), (), [3 + i])
+        E("v", lambda e: e.memset(T["Vt%d" % i][:, 0:16], 0.0), (), [("Vt", i)])
+    E("v", lambda e: e.memset(T.u3[:], 1.0), (), ["u3"])
+    cts("ki", "pc", 15, None, A.bitwise_and)
+    cts("gi", "pc", 4, None, A.arith_shift_right)
+    cts("Jk", "J", 15, None, A.bitwise_and)
+    cts("Jg", "J", 4, None, A.arith_shift_right)
+    colv(P_, "pc", 0.0, None, A.add)
+    colv(G_, "gi", 0.0, None, A.add)
+    colv(DBI, "ki", 7.0, -127.5, A.is_equal, A.mult)
+    cts("ID", "J", c1(P_), None, A.is_equal, None, [P_])
+    cts("BO", "Jg", c1(G_), None, A.is_equal, None, [G_])
+    cts("u1", "Jk", 15.0, -16.0, A.is_equal, A.mult)
+    cts("u2", "Jk", 7.0, 1000.0, A.is_equal, A.mult)
+    ctt("u1", "u1", "u2", A.add)
+    ctt("u1", "u1", "J", A.add)
+    cts("u2", "u1", 1.0, c1(P_), A.add, A.is_equal, [P_])
+    ctt("DM", "ID", "u2", A.subtract)
+    act(T.ID16[:], T.ID[:], ["ID"], ["ID16"])
+    act(T.NID[:], T.ID[:], ["ID"], ["NID"], scale=-1.0)
+    act(T.NID16[:], T.ID[:], ["ID"], ["NID16"], scale=-1.0)
+    act(T.BOf[:], T.BO[:], ["BO"], ["BOf"])
+    act(T.C16[:], T.u3[:], ["u3"], ["C16"], scale=16.0)
+    for i in range(4):
+        act(T.ON16[:, 128 * i:128 * i + 128], T.u3[:], ["u3"], ["ON16"])
+    colv(K_, "ki", 0.0, None, A.add)
+    cts("si", "ki", 8.0, None, A.add)
+    cts("si", "si", 15, None, A.bitwise_and)
+    colv(S_, "si", 0.0, None, A.add)
+    cts("S8", "K8", 8.0, None, A.add)
+    cts("S8", "S8", 15, None, A.bitwise_and)
+    cts("v1", "G8", c1(G_), None, A.is_equal, None, [G_])
+    cts("v2", "S8", c1(S_), None, A.is_le, None, [S_])
+    ctt("EK", "v1", "v2", A.mult)
+    for h in (0, 1):
+        cp(T.cU_0[:, 256 * h:256 * h + 256], T.ci[:, h::2], ["ci"], [("cU", 0, 2 * h), ("cU", 0, 2 * h + 1)])
+    cts("wb", "wi", 0.0, None, A.add)
+    colv(WF, "wi", 0.0, None, A.add)
+    cts("BW", "BO", c1(WF), None, A.mult, None, [WF])
+    for o, i in (("LO", "BO"), ("LW", "BW")):
+        for q in range(16):
+            E("g", lambda e: e.affine_select(T[o][:, 128 * q:128 * q + 128], T[i][:], [[0, 8], [1, 16]], A.is_equal, 0.0, -q, 0),
+              [i], [(o, q)])
+    colv(K1, "ki", 1.0, None, A.add)
+    colv(IS15, "ki", 15.0, None, A.is_equal)
+    colv(WSC, "ki", 15.0, None, A.not_equal)
+    cts("Js", "J", 8.0, None, A.add)
+    cts("Js", "Js", 15, None, A.bitwise_and)
+    cts("u1", "Js", -7.0, 512.0, A.add, A.mult)
+    cts("u1", "u1", c1(IS15), c1(WSC), A.mult, A.add, [IS15, WSC])
+    ctt("BS", "u1", "BO", A.mult)
+    cts("colk", "K16", c1(K1), -512.0, A.is_equal, A.mult, [K1])
+    cts("colk", "colk", c1(IS15), None, A.add, None, [IS15])
+    for k in range(1, 16):
+        ts(T.PL[:, 128 * k:128 * k + 128], T.BS[:], T.colk[:, k:k + 1], None, A.mult, None, ["BS", "colk"], [("PL", k)])
+    colv(P1, "pc", 1.0, None, A.add)
+    cts("u1", "J", c1(P1), None, A.is_equal, None, [P1])
+    ctt("u2", "u1", "BO", A.mult)
+    cts("SH", "u2", 256.0, None, A.mult)
+    ctt("DC", "ID", "u2", A.subtract)
+    cts("u1", "Jk", 1.0, 14400.0, A.is_ge, A.mult)
+    ctt("u1", "u1", "BO", A.mult)
+    cts("v1", "u1", c1(IS15), None, A.mult, None, [IS15])
+    cts("v2", "u2", 3840.0, None, A.mult)
+    ctt("CW", "v1", "v2", A.add)
+    colv(THR, "ki", 0.0, 1.0e6, A.is_equal, A.mult)
+    ts(c1(NTHR), c1(THR), -1.0, -96.25, A.mult, A.add, [("col", THR)], [("col", NTHR)])
+    ts(c1(THR), c1(THR), 96.25, None, A.add, None, [("col", THR)], [("col", THR)])
+
+    for i in range(8):
+        sl, X = slice(512 * i, 512 * i + 512), (0, 1, 2, 5, 6, 7)[i % 6]
+        mm(ps[X][:], T.DM[:], T.xin[:, sl], True, True, ["DM", ("xin", i // 2)], X)
+        if i in (3, 5, 7):
+            ts(T.Dt[:, sl], ps[X][:], c1(DBI), None, A.add, None, [("col", DBI)], [("Dt", i)], [X])
+        else:
+            act(T.Dt[:, sl], ps[X][:], [("col", DBI)], [("Dt", i)], [X], bias=c1(DBI))
+    Dk = [("Dt", i) for i in range(8)]
+    Bk = [("Bt", i) for i in range(4)]
+
+    def unpack(h):
+        i = T.pin[:, 1024 * h:1024 * h + 1024]
+        ts(T.Bt[:, 1024 * h:1024 * h + 1024], i, 4095, None, A.bitwise_and, None, [("pin", h)], [("Bt", h)])
+        ts(T.Bt[:, 2048 + 1024 * h:3072 + 1024 * h], i, 12, None, A.arith_shift_right, None, [("pin", h)], [("Bt", 2 + h)])
+
+    def late_constants():
+        mm(ps[4][:, 300:301], T.BO[:], T.wb[:], True, True, ["BO", "wb"], 4)
+        ts(c1(H0), ps[4][:, 300:301], 127.5, None, A.mult, None, (), [("col", H0)], [4])
+        colv(G32, "gi", 32.0, None, A.mult)
+        colv(G16, "gi", 16.0, None, A.mult)
+        cts("iL", "iL0", c1(G32), None, A.subtract, None, [G32])
+        cts("mL", "mL0", c1(G16), None, A.subtract, None, [G16])
+        cts("u1", "K8", c1(K_), None, A.is_equal, None, [K_])
+        cts("u2", "G8", c1(G_), None, A.is_equal, None, [G_])
+        ctt("DK", "u1", "u2", A.mult)
+        cts("u1", "Js", c1(S_), None, A.is_le, None, [S_])
+        ctt("SX", "u1", "BO", A.mult)
+
+    ones = T.EK[:, 64:72]
+
+    def keys(n, a, m):
+        return [(n, x) for x in range(a // 16, (a + m) // 16)]
+
+    def gath(q, dst, win, t, a, n, R, Wk, bias=0.0):
+        w = win.indirect(T["cU_%d" % t][:, a:a + n])
+        out = dst[:, 16 * a:16 * (a + n)]
+        R = R + [("cU", t, x) for x in range(a // 128, (a + n + 127) // 128)]
+        if q == "s":
+            act(out, w, R, Wk, bias=bias)
+        elif bias:
+            ts(out, w, bias, None, A.add, None, R, Wk)
+        else:
+            cp(out, w, R, Wk)
+
+    def xg(q, t, a, n):
+        gath(q, T.G, T.Dt[:, 0:W], t, a, n, Dk, keys("G", a, n))
+
+    def bg(q, t, a, n):
+        gath(q, T.GB, T.Bt[:, 0:W], t, a, n, Bk, keys("GB", a, n), -2048.0)
+
+    def Gk(b):
+        return keys("G", 128 * b, 128)
+
+    def ediag(b):
+        X = 3 + b % 2
+        for k in range(15):
+            mm(ps[X][:, k:128:16], T.G[:, 2048 * b + k:2048 * b + 2048:16], T.EK[:, 8 * k:8 * k + 8], True, True, Gk(b) + ["EK"], X)
+
+    def zone1(b):
+        X, h, i = 3 + b % 2, 128 * (b % 2), b % 2
+        C = 1.5 * 2.0 ** 27
+        ts(T.R1[:, h:h + 128], ps[X][:, 0:128], C, C, A.add, A.subtract, (), [("R1", i)], [X])
+        tt(T.wT[:, h:h + 128], ps[X][:, 0:128], T.R1[:, h:h + 128], A.subtract, [("R1", i)], [("wT", i)], [X])
+
+    def zone2(b):
+        X, h, i = 3 + b % 2, 128 * (b % 2), b % 2
+        mm(ps[X][:, 128:256], T.wT[:, h:h + 128], T.ID[:], True, True, [("wT", i), "ID"], X)
+
+    def zone3(b):
+        X, h, i = 3 + b % 2, 128 * (b % 2), b % 2
+        ts(T.Wz[:, h:h + 128], ps[X][:, 128:256], c1(WSC), c1(IS15), A.mult, A.add, [("col", WSC), ("col", IS15)], [("Wz", i)], [X])
+        tt(T.W2[:, h:h + 128], ps[X][:, 128:256], T.Wz[:, h:h + 128], A.mult, [("Wz", i)], [("W2", i)], [X])
+
+    CH = ((1, 2, 3, 4), (5, 6, 7, 8), (9, 10, 11, 12), (13, 14, 15))
+
+    def pen(b, c):
+        X, h = (4 * b + c) % 3, 128 * (b % 2)
+        for i, k in enumerate(CH[c]):
+            mm(ps[X][:, 128 * i:128 * i + 128], T.PL[:, 128 * k:128 * k + 128], T.Wz[:, h:h + 128], True, True,
+               [("PL", k), ("Wz", b % 2)], X)
+
+    def sel(b, c):
+        X, h = (4 * b + c) % 3, 2048 * (b % 2)
+        for i, k in enumerate(CH[c]):
+            tt(T.VM[:, h + 128 * k:h + 128 * k + 128], T.G[:, 2048 * b + k:2048 * b + 2048:16], ps[X][:, 128 * i:128 * i + 128],
+               A.min, Gk(b), [("VM", b % 2, k)], [X])
+
+    def corr(b):
+        X, h, i = 5 + b % 2, 128 * (b % 2), b % 2
+        mm(ps[X][:, 0:128], T.Wz[:, h:h + 128], T.CW[:], True, False, [("Wz", i), "CW"], X)
+        mm(ps[X][:, 0:128], T.W2[:, h:h + 128], T.SH[:], False, False, [("W2", i), "SH"], X)
+        mm(ps[X][:, 0:128:16], T.G[:, 2048 * b:2048 * b + 2048:16], T.EK[:, 0:8], False, False, Gk(b) + ["EK"], X)
+
+    def sums(b, c):
+        X, h = 5 + b % 2, 2048 * (b % 2)
+        for k in CH[c]:
+            mm(ps[X][:, k:128:16], T.VM[:, h + 128 * k:h + 128 * k + 128], ones, False, k == 15, [("VM", b % 2, k), "EK"], X)
+
+    def vcopy(b):
+        X = 5 + b % 2
+        cp(T["Vt%d" % (b % 2)][:, 1:129], ps[X][:, 0:128], (), [("Vt", b % 2)], [X])
+
+    def turn(b):
+        X, V, K = 5 + b % 2, T["Vt%d" % (b % 2)], [("Vt", b % 2)]
+        if b == 3:
+            mm(ps[X][:, 256:384], V[:, 1:129], T.ID[:], True, False, K + ["ID"], X)
+            mm(ps[X][:, 256:384], V[:, 0:128], T.NID[:], False, True, K + ["NID"], X)
+        mm(ps[X][:, 128:256], V[:, 1:129], T.ID[:], True, True, K + ["ID"], X)
+
+    def vs(b):
+        X, j = 5 + b % 2, 128 * b
+        cp(T.VS[:, j:j + 128], ps[X][:, 128:256], (), [("VS", b)], [X])
+
+    def diff(b):
+        X, j = 5 + b % 2, 128 * b
+        mm(ps[X][:, 256:384], T.DC[:], T.VS[:, j:j + 128], True, True, [("VS", b), "DC"], X)
+
+    def cracks(b):
+        X, j = 5 + b % 2, 128 * b
+        ts(T.CC[:, j:j + 128], ps[X][:, 256:384], c1(THR), None, A.is_gt, None, [("col", THR)], [("CC", b)], [X])
+        ts(T.CC[:, 512 + j:640 + j], ps[X][:, 256:384], c1(NTHR), None, A.is_lt, None, [("col", NTHR)], [("CD", b)], [X])
+
+    def crack(b):
+        j = 128 * b
+        tt(T.cr[:, j:j + 128], T.CC[:, j:j + 128], T.CC[:, 512 + j:640 + j], A.add, [("CC", b), ("CD", b)], [("cr", b)])
+
+    VSk = [("VS", b) for b in range(4)]
+    CCk = [("CC", b) for b in range(4)] + [("CD", b) for b in range(4)]
+    sent = [0]
+
+    def send(t, out, src, R):
+        to = T.cores[(rank + 1 + t % 3) % len(T.cores)]
+        eg = topo.engines(core, to)[:8]
+        rid, pid, _ = topo.addr(to)
+        waits("g", [wr[k] for k in R])
+        g.remote_dma(out, src, T.sem["arr%d" % t], T.sem.loc, pid, rid, sum(1 << x for x in eg))
+        sent[0] += len(eg)
+        return len(eg)
+
+    for t in range(ROUNDS):
+        cU, c16, Dn, pU = T["cU_%d" % t], T["c16_%d" % t], T["Dn_%d" % t], T["pU_%d" % t]
+        C16 = [("c16", t)]
+        xg("s", t, 48, 80)
+        xg("v", t, 0, 48)
+        xg("v", t, 128, 32)
+        xg("s", t, 160, 96)
+        xg("s", t, 256, 128)
+        xg("s", t, 384, 128)
+        send(t, T["rC_%d" % t][:], cU[:, 256:512], [("cU", t, x) for x in range(4)])
+        ediag(0)
+        zone1(0)
+        zone2(0)
+        zone3(0)
+        ts(c16[:], cU[:], -2048.0, None, A.add, None, [("cU", t, x) for x in range(4)], C16)
+        for b in range(NB):
+            pen(b, 0)
+            pen(b, 1)
+            sel(b, 0)
+            if b:
+                turn(b - 1)
+                vs(b - 1)
+            sel(b, 1)
+            if b:
+                diff(b - 1)
+            pen(b, 2)
+            if b:
+                cracks(b - 1)
+            sel(b, 2)
+            if b:
+                crack(b - 1)
+            if b < 3:
+                ediag(b + 1)
+                zone1(b + 1)
+            corr(b)
+            sums(b, 0)
+            pen(b, 3)
+            sel(b, 3)
+            sums(b, 1)
+            sums(b, 2)
+            if b < 3:
+                zone2(b + 1)
+                zone3(b + 1)
+            sums(b, 3)
+            vcopy(b)
+            if t == 0 and b < 3:
+                (lambda: unpack(0), lambda: unpack(1), late_constants)[b]()
+        for b in range(NB):
+            bg("s", t, 128 * b, 128)
+        turn(3)
+        cracks(3)
+        vs(3)
+        crack(3)
+        for q in range(16):
+            mm(ps[7][:, 64:128], T.LO[:, 128 * q:128 * q + 128], T.CC[:, q::16], q == 0, q == 15, CCk + [("LO", q)], 7)
+        mm(ps[0][:, 0:256], T.DM[:], T.VS[:, 256:512], True, True, VSk + ["DM"], 0)
+        for q in range(16):
+            mm(ps[3][:, 256:288], T.LW[:, 128 * q:128 * q + 128], T.VS[:, q::16], q == 0, q == 15, VSk + [("LW", q)], 3)
+        E("v", lambda e: e.tensor_reduce(T.Rr[:], ps[7][:, 64:128], AxisListType.X, A.add), (), ["Rr"], [7])
+        cp(T.n2s[:], ps[7][:, 96:128], (), ["n2s"], [7])
+        mm(ps[4][:, 256:257], T.BOf[:], T.Rr[:], True, True, ["BOf", "Rr"], 4)
+        mm(ps[1][:, 0:256], T.DM[:], T.VS[:, 0:256], True, True, VSk + ["DM"], 1)
+        cp(Dn[:, 256:512], ps[0][:, 0:256], (), [("Dn", t, 1)], [0])
+        send(t, T["rD_%d" % t][:], Dn[:, 256:512], [("Dn", t, 1)])
+        tt(T.nn[:], ps[7][:, 64:96], T.n2s[:], A.add, ["n2s"], ["nn"], [7])
+        cts("na", "nn", 5.5, float(DUMP), A.is_gt, A.mult)
+        ctt("rp", "na", "iL", A.add)
+        ts(T.Hs[:], ps[3][:, 256:288], c1(H0), None, A.add, None, [("col", H0)], ["Hs"], [3])
+        Ac = ps[4][:, 256:257]
+        ts(T.i1[:], T.Hs[:], Ac, 512.0, A.add, A.mult, ["Hs"], ["i1"], [4])
+        cts("i2", "i1", 3584, None, A.bitwise_and)
+        ctt("pf", "i2", "rp", A.add)
+        cp(pU[:], T.pf[:], ["pf"], [("pU", t)])
+        ne = 3 * send(t, T["rP_%d" % t][:], pU[:, 16:32], [("pU", t)])
+        mm(ps[6][:], T.ID16[:], c16[:], True, False, C16 + ["ID16"], 6)
+        mm(ps[6][:], T.C16[:], T.ON16[:], False, True, ["C16", "ON16"], 6)
+
+        def bdiag(b):
+            X = (2, 3)[b % 2]
+            for k in range(1, 16):
+                mm(ps[X][:, k:128:16], T.GB[:, 2048 * b + k:2048 * b + 2048:16], T.DK[:, 8 * k:8 * k + 8], True, True,
+                   keys("GB", 128 * b, 128) + ["DK"], X)
+
+        def bturn(b):
+            s = slice(128 * b, 128 * b + 128)
+            act(T.BT[:, s], ps[(2, 3)[b % 2]][:, 0:128], (), [("BT", b)], [(2, 3)[b % 2]])
+            mm(ps[5][:, s], T.BT[:, s], T.ID16[:], True, False, [("BT", b), "ID16"], 5)
+            mm(ps[5][:, s], T.NID16[:], c16[:, s], False, True, C16 + ["NID16"], 5)
+
+        bdiag(0)
+        for b in range(NB):
+            if b < 3:
+                bdiag(b + 1)
+            bturn(b)
+        cp(Dn[:, 0:256], ps[1][:, 0:256], (), [("Dn", t, 0)], [1])
+        ts(T.x1[:], T.Hs[:], 37.0, Ac, A.mult, A.add, ["Hs"], ["x1"], [4])
+        cts("x2", "x1", 4095, None, A.bitwise_and)
+        cts("na1", "nn", 5.5, None, A.is_gt)
+        ctt("y1", "mL", "x2", A.subtract)
+        ctt("y2", "y1", "na1", A.mult)
+        ctt("y3", "y2", "x2", A.add)
+        cp(T.nx[:], T.y3[:], ["y3"], ["nx"])
+        cp(T.Dt[:].indirect(pU[:, 0:16]), Dn[:, 0:256], [("pU", t), ("Dn", t, 0)], Dk)
+        cp(T.Bt[:].indirect(pU[:, 0:16]), cU[:, 0:256], [("pU", t), ("cU", t, 0), ("cU", t, 1)], Bk + ["Bm"])
+        wr[("arr", t)] = ("arr%d" % t, ne)
+        rP = T["rP_%d" % t][:]
+        win = T.Bt[:, 0:DUMP]
+        B5 = Bk + ["Bm", "nx"]
+
+        def rscat(w):
+            if w:
+                cp(T.Dt[:].indirect(rP), T["rD_%d" % t][:], [("arr", t)], Dk)
+            else:
+                cp(T.Bt[:].indirect(rP), T["rC_%d" % t][:], [("arr", t)], Bk + ["Bm"])
+
+        rscat(t == ROUNDS - 1)
+        rscat(t < ROUNDS - 1)
+        tt(T.t2[:], ps[5][:], T.cr[:], A.mult, [("cr", b) for b in range(4)], ["t2"], [5])
+        tt(T.Bt[:, MEND:MEND + 512], T.t2[:], ps[6][:], A.add, ["t2"], ["Bm"], [6])
+        if t < ROUNDS - 1:
+            nU = T["cU_%d" % (t + 1)]
+            cp(nU[:, 0:128], win.indirect(T.nx[:, 0:8]), B5, [("cU", t + 1, 0)])
+            cp(nU[:, 128:512], win.indirect(T.nx[:, 8:32]), B5, [("cU", t + 1, x) for x in (1, 2, 3)])
+        else:
+            for h in (0, 1):
+                cp(T.ycs[:, h::2], win.indirect(T.nx[:, 16 * h:16 * h + 16]), B5, [("yc", h)])
+
+    for i in range(8):
+        sl = slice(512 * i, 512 * i + 512)
+        mm(ps[i][:], T.SX[:], T.Dt[:, sl], True, True, Dk + ["SX"], i)
+        if i % 2:
+            E("s", lambda e: e.activation(T.xin[:, sl], ps[i][:], F.Copy, bias=127.5), (), [("xo", i)], [i])
+            c = slice(512 * (i - 1), 512 * (i + 1))
+            DMA("y", T.yx[:, c], T.xin[:, c], "o%d" % (i // 2), [("xo", i - 1), ("xo", i)])
+        else:
+            ts(T.xin[:, sl], ps[i][:], 127.5, None, A.add, None, (), [("xo", i)], [i])
+    DMA("s", T.yc[:], T.ycs[:], "o4", [("yc", 0), ("yc", 1)])
+    waits("g", [(s_, 16) for s_ in SEMAPHORES if s_[0] == "o" or (s_[0] == "l" and s_ != "loc")])
+    waits("g", [("loc", sent[0])] + [(qsem[q], cnt[q]) for q in qsem])

@@ -10,12 +10,12 @@ DUMP = 4608
 WIN = DUMP + 4096
 LONG = {"f": "float32", "b": "bfloat16", "h": "float16", "i": "int32", "u": "uint16"}
 SCRATCH = {}
-_spec = """Dt:8704b Bt:8704i xin:4096b pin:2048i ci:512i wi:1i G:8192b GB:8192h VM:4096b R1:256f wT:256b Wz:256b W2:256b
-Vt0:144b Vt1:144b VS:512b CC:1024b cr:512b BT:512h t2:512f ycs:512f Rr:1f Hs:32f n2s:32f nn:32f na:32f na1:32f rp:32f
-i1:32i i2:32i pf:32f x1:32i x2:32i y1:32f y2:32f y3:32f nx:32u pc:1i ki:1i gi:1i si:1i col:32f wb:1b J:128i Jk:128i Js:128i
-Jg:128i K8:128i S8:128i G8:128i K16:16i iL:32f mL:32f iL0:32i mL0:32i u1:128f u2:128f u3:128f v1:128f v2:128f colk:16f
-BO:128b BW:128b BOf:128f BS:128b ID:128b NID:128b ID16:128h NID16:128h C16:128h ON16:512h EK:128b DK:128h DM:128b DC:128b SX:128b
-SH:128b CW:128b PL:2048b LO:2048b LW:2048b"""
+_spec = """Dt:8704b Bt:8704i xin:4096b pin:2048i ci:512i wi:1i G:8192b GB:8192h VM:4096b R1:256f wT:256b Wz:256b SQ0:136f SQ1:136f
+Vt0:144b Vt1:144b VS:512b CC:512b nd:128b ad:128b BT:512h t2:512f ycs:512f Rr:1f Hs:32f na:32f na1:32f rp:32f
+i1:32i i2:32i pf:32f x1:32i x2:32i y1:32f y3:32f nx:32u pc:1i ki:1i gi:1i si:1i col:32f wb:1b J:128i Jk:128i Js:128i
+Jg:128i K8:128i S8:128i G8:128i K16:16i iL:32f mL:32f iL0:32i mL0:32i u1:128f u2:128f v1:128f v2:128f colk:16f
+BO:128b BW:128b BOf:128f BS:128b ID:128b NID:128b ID16:128h NID16:128h EK:128b DK:128h DM:128b DC:128b SX:128b
+PL:2048b LO:2048b LW:2048b"""
 for _t in range(ROUNDS):
     _spec += " cU_%d:512u c16_%d:512h Dn_%d:512b pU_%d:32u rC_%d:256u rD_%d:256b rP_%d:16u" % ((_t,) * 7)
 for _w in _spec.split():
@@ -24,7 +24,7 @@ for _w in _spec.split():
 for _t in range(8):
     SCRATCH["ps%d" % _t] = ("psum", [128, 512], "float32")
 SEMAPHORES = "qv qs qt qg loc lci lwt lx0 lx1 lx2 lx3 lp0 lp1 arr0 arr1 arr2 arr3 o0 o1 o2 o3 o4".split()
-K_, G_, S_, P_, P1, G16, G32, IS15, WSC, THR, NTHR, DBI, H0, WF, K1 = range(15)
+K_, G_, S_, P_, P1, G16, G32, IS15, WSC, THR, DBI, H0, WF, K1 = range(14)
 
 
 def rank_program(g, core, T, topo):
@@ -124,103 +124,92 @@ def rank_program(g, core, T, topo):
                                ("iL0", [[1, 2], [32, 16]], 0, 2), ("mL0", [[16, 32]], MEND, 1)):
         E("g", lambda e: e.iota(T[buf][:], pat, base, cm), (), [buf])
     for i in (0, 1):
-        E("v", lambda e: e.memset(ps[3 + i][:, 0:128], 0.0), (), (), [3 + i])
+        E("v", lambda e: e.memset(ps[3 + i][:, 0:128], -7.5), (), (), [3 + i])
         E("v", lambda e: e.memset(T["Vt%d" % i][:, 0:16], 0.0), (), [("Vt", i)])
-    E("v", lambda e: e.memset(T.u3[:], 1.0), (), ["u3"])
+        E("v", lambda e: e.memset(T["SQ%d" % i][:, 0:8], 0.0), (), [("SQ", i)])
     cts("ki", "pc", 15, None, A.bitwise_and)
     cts("gi", "pc", 4, None, A.arith_shift_right)
     cts("Jk", "J", 15, None, A.bitwise_and)
     cts("Jg", "J", 4, None, A.arith_shift_right)
     colv(P_, "pc", 0.0, None, A.add)
+    colv(P1, "pc", 1.0, None, A.add)
     colv(G_, "gi", 0.0, None, A.add)
-    colv(DBI, "ki", 7.0, -127.5, A.is_equal, A.mult)
-    cts("ID", "J", c1(P_), None, A.is_equal, None, [P_])
-    cts("BO", "Jg", c1(G_), None, A.is_equal, None, [G_])
     cts("u1", "Jk", 15.0, -16.0, A.is_equal, A.mult)
     cts("u2", "Jk", 7.0, 1000.0, A.is_equal, A.mult)
+    colv(DBI, "ki", 7.0, -127.5, A.is_equal, A.mult)
+    cts("ID", "J", c1(P_), None, A.is_equal, None, [P_])
     ctt("u1", "u1", "u2", A.add)
+    cts("BO", "Jg", c1(G_), None, A.is_equal, None, [G_])
+    cts("si", "ki", 8.0, None, A.add)
+    cts("S8", "K8", 8.0, None, A.add)
     ctt("u1", "u1", "J", A.add)
+    cts("Js", "J", 8.0, None, A.add)
+    cts("si", "si", 15, None, A.bitwise_and)
+    cts("S8", "S8", 15, None, A.bitwise_and)
     cts("u2", "u1", 1.0, c1(P_), A.add, A.is_equal, [P_])
+    cts("Js", "Js", 15, None, A.bitwise_and)
+    colv(S_, "si", 0.0, None, A.add)
     ctt("DM", "ID", "u2", A.subtract)
+    cts("v1", "G8", c1(G_), None, A.is_equal, None, [G_])
+    cts("v2", "S8", c1(S_), None, A.is_le, None, [S_])
+    cts("wb", "wi", 0.0, None, A.add)
+    colv(WF, "wi", 0.0, None, A.add)
+    ctt("EK", "v1", "v2", A.mult)
     act(T.ID16[:], T.ID[:], ["ID"], ["ID16"])
     act(T.NID[:], T.ID[:], ["ID"], ["NID"], scale=-1.0)
     act(T.NID16[:], T.ID[:], ["ID"], ["NID16"], scale=-1.0)
     act(T.BOf[:], T.BO[:], ["BO"], ["BOf"])
-    act(T.C16[:], T.u3[:], ["u3"], ["C16"], scale=16.0)
-    for i in range(4):
-        act(T.ON16[:, 128 * i:128 * i + 128], T.u3[:], ["u3"], ["ON16"])
-    colv(K_, "ki", 0.0, None, A.add)
-    cts("si", "ki", 8.0, None, A.add)
-    cts("si", "si", 15, None, A.bitwise_and)
-    colv(S_, "si", 0.0, None, A.add)
-    cts("S8", "K8", 8.0, None, A.add)
-    cts("S8", "S8", 15, None, A.bitwise_and)
-    cts("v1", "G8", c1(G_), None, A.is_equal, None, [G_])
-    cts("v2", "S8", c1(S_), None, A.is_le, None, [S_])
-    ctt("EK", "v1", "v2", A.mult)
-    for h in (0, 1):
-        cp(T.cU_0[:, 256 * h:256 * h + 256], T.ci[:, h::2], ["ci"], [("cU", 0, 2 * h), ("cU", 0, 2 * h + 1)])
-    cts("wb", "wi", 0.0, None, A.add)
-    colv(WF, "wi", 0.0, None, A.add)
     cts("BW", "BO", c1(WF), None, A.mult, None, [WF])
     for o, i in (("LO", "BO"), ("LW", "BW")):
         for q in range(16):
             E("g", lambda e: e.affine_select(T[o][:, 128 * q:128 * q + 128], T[i][:], [[0, 8], [1, 16]], A.is_equal, 0.0, -q, 0),
               [i], [(o, q)])
+    colv(K_, "ki", 0.0, None, A.add)
     colv(K1, "ki", 1.0, None, A.add)
     colv(IS15, "ki", 15.0, None, A.is_equal)
     colv(WSC, "ki", 15.0, None, A.not_equal)
-    cts("Js", "J", 8.0, None, A.add)
-    cts("Js", "Js", 15, None, A.bitwise_and)
     cts("u1", "Js", -7.0, 512.0, A.add, A.mult)
-    cts("u1", "u1", c1(IS15), c1(WSC), A.mult, A.add, [IS15, WSC])
-    ctt("BS", "u1", "BO", A.mult)
     cts("colk", "K16", c1(K1), -512.0, A.is_equal, A.mult, [K1])
+    cts("u2", "J", c1(P1), None, A.is_equal, None, [P1])
+    cts("u1", "u1", c1(IS15), c1(WSC), A.mult, A.add, [IS15, WSC])
     cts("colk", "colk", c1(IS15), None, A.add, None, [IS15])
+    ctt("u2", "u2", "BO", A.mult)
+    ctt("BS", "u1", "BO", A.mult)
+    colv(THR, "ki", 0.0, 1.0e6, A.is_equal, A.mult)
+    ctt("DC", "ID", "u2", A.subtract)
     for k in range(1, 16):
         ts(T.PL[:, 128 * k:128 * k + 128], T.BS[:], T.colk[:, k:k + 1], None, A.mult, None, ["BS", "colk"], [("PL", k)])
-    colv(P1, "pc", 1.0, None, A.add)
-    cts("u1", "J", c1(P1), None, A.is_equal, None, [P1])
-    ctt("u2", "u1", "BO", A.mult)
-    cts("SH", "u2", 256.0, None, A.mult)
-    ctt("DC", "ID", "u2", A.subtract)
-    cts("u1", "Jk", 1.0, 14400.0, A.is_ge, A.mult)
-    ctt("u1", "u1", "BO", A.mult)
-    cts("v1", "u1", c1(IS15), None, A.mult, None, [IS15])
-    cts("v2", "u2", 3840.0, None, A.mult)
-    ctt("CW", "v1", "v2", A.add)
-    colv(THR, "ki", 0.0, 1.0e6, A.is_equal, A.mult)
-    ts(c1(NTHR), c1(THR), -1.0, -96.25, A.mult, A.add, [("col", THR)], [("col", NTHR)])
     ts(c1(THR), c1(THR), 96.25, None, A.add, None, [("col", THR)], [("col", THR)])
+    for h in (0, 1):
+        cp(T.cU_0[:, 256 * h:256 * h + 256], T.ci[:, h::2], ["ci"], [("cU", 0, 2 * h), ("cU", 0, 2 * h + 1)])
+    mm(ps[4][:, 300:301], T.BO[:], T.wb[:], True, True, ["BO", "wb"], 4)
+    colv(G32, "gi", 32.0, None, A.mult)
+    colv(G16, "gi", 16.0, None, A.mult)
+    cts("u1", "K8", c1(K_), None, A.is_equal, None, [K_])
+    cts("u2", "Js", c1(S_), None, A.is_le, None, [S_])
+    cts("iL", "iL0", c1(G32), None, A.subtract, None, [G32])
+    cts("mL", "mL0", c1(G16), None, A.subtract, None, [G16])
+    ctt("DK", "u1", "v1", A.mult)
+    ctt("SX", "u2", "BO", A.mult)
+    ts(c1(H0), ps[4][:, 300:301], 127.5, None, A.mult, None, (), [("col", H0)], [4])
 
     for i in range(8):
         sl, X = slice(512 * i, 512 * i + 512), (0, 1, 2, 5, 6, 7)[i % 6]
         mm(ps[X][:], T.DM[:], T.xin[:, sl], True, True, ["DM", ("xin", i // 2)], X)
-        if i in (3, 5, 7):
+        if i in (3, 7):
             ts(T.Dt[:, sl], ps[X][:], c1(DBI), None, A.add, None, [("col", DBI)], [("Dt", i)], [X])
         else:
             act(T.Dt[:, sl], ps[X][:], [("col", DBI)], [("Dt", i)], [X], bias=c1(DBI))
     Dk = [("Dt", i) for i in range(8)]
-    Bk = [("Bt", i) for i in range(4)]
+    Bk = [("Bt", i) for i in range(8)]
 
-    def unpack(h):
-        i = T.pin[:, 1024 * h:1024 * h + 1024]
-        ts(T.Bt[:, 1024 * h:1024 * h + 1024], i, 4095, None, A.bitwise_and, None, [("pin", h)], [("Bt", h)])
-        ts(T.Bt[:, 2048 + 1024 * h:3072 + 1024 * h], i, 12, None, A.arith_shift_right, None, [("pin", h)], [("Bt", 2 + h)])
+    def unpack(i):
+        s, n = i // 2, 1024 * (i // 2) + 512 * (i % 2)
+        j = T.pin[:, n:n + 512]
+        ts(T.Bt[:, n:n + 512], j, 4095, None, A.bitwise_and, None, [("pin", s)], [("Bt", i)])
+        ts(T.Bt[:, 2048 + n:2560 + n], j, 12, None, A.arith_shift_right, None, [("pin", s)], [("Bt", 4 + i)])
 
-    def late_constants():
-        mm(ps[4][:, 300:301], T.BO[:], T.wb[:], True, True, ["BO", "wb"], 4)
-        ts(c1(H0), ps[4][:, 300:301], 127.5, None, A.mult, None, (), [("col", H0)], [4])
-        colv(G32, "gi", 32.0, None, A.mult)
-        colv(G16, "gi", 16.0, None, A.mult)
-        cts("iL", "iL0", c1(G32), None, A.subtract, None, [G32])
-        cts("mL", "mL0", c1(G16), None, A.subtract, None, [G16])
-        cts("u1", "K8", c1(K_), None, A.is_equal, None, [K_])
-        cts("u2", "G8", c1(G_), None, A.is_equal, None, [G_])
-        ctt("DK", "u1", "u2", A.mult)
-        cts("u1", "Js", c1(S_), None, A.is_le, None, [S_])
-        ctt("SX", "u1", "BO", A.mult)
-
+    BM, MB = [("Bm", 0), ("Bm", 2)], (5, 5, 0, 0)
     ones = T.EK[:, 64:72]
 
     def keys(n, a, m):
@@ -254,8 +243,8 @@ def rank_program(g, core, T, topo):
     def zone1(b):
         X, h, i = 3 + b % 2, 128 * (b % 2), b % 2
         C = 1.5 * 2.0 ** 27
-        ts(T.R1[:, h:h + 128], ps[X][:, 0:128], C, C, A.add, A.subtract, (), [("R1", i)], [X])
-        tt(T.wT[:, h:h + 128], ps[X][:, 0:128], T.R1[:, h:h + 128], A.subtract, [("R1", i)], [("wT", i)], [X])
+        return [lambda: ts(T.R1[:, h:h + 128], ps[X][:, 0:128], C, C, A.add, A.subtract, (), [("R1", i)], [X]),
+                lambda: tt(T.wT[:, h:h + 128], ps[X][:, 0:128], T.R1[:, h:h + 128], A.subtract, [("R1", i)], [("wT", i)], [X])]
 
     def zone2(b):
         X, h, i = 3 + b % 2, 128 * (b % 2), b % 2
@@ -264,7 +253,6 @@ def rank_program(g, core, T, topo):
     def zone3(b):
         X, h, i = 3 + b % 2, 128 * (b % 2), b % 2
         ts(T.Wz[:, h:h + 128], ps[X][:, 128:256], c1(WSC), c1(IS15), A.mult, A.add, [("col", WSC), ("col", IS15)], [("Wz", i)], [X])
-        tt(T.W2[:, h:h + 128], ps[X][:, 128:256], T.Wz[:, h:h + 128], A.mult, [("Wz", i)], [("W2", i)], [X])
 
     CH = ((1, 2, 3, 4), (5, 6, 7, 8), (9, 10, 11, 12), (13, 14, 15))
 
@@ -274,33 +262,38 @@ def rank_program(g, core, T, topo):
             mm(ps[X][:, 128 * i:128 * i + 128], T.PL[:, 128 * k:128 * k + 128], T.Wz[:, h:h + 128], True, True,
                [("PL", k), ("Wz", b % 2)], X)
 
-    def sel(b, c):
+    def sel(b, c, later=False):
         X, h = (4 * b + c) % 3, 2048 * (b % 2)
-        for i, k in enumerate(CH[c]):
-            tt(T.VM[:, h + 128 * k:h + 128 * k + 128], T.G[:, 2048 * b + k:2048 * b + 2048:16], ps[X][:, 128 * i:128 * i + 128],
-               A.min, Gk(b), [("VM", b % 2, k)], [X])
-
-    def corr(b):
-        X, h, i = 5 + b % 2, 128 * (b % 2), b % 2
-        mm(ps[X][:, 0:128], T.Wz[:, h:h + 128], T.CW[:], True, False, [("Wz", i), "CW"], X)
-        mm(ps[X][:, 0:128], T.W2[:, h:h + 128], T.SH[:], False, False, [("W2", i), "SH"], X)
-        mm(ps[X][:, 0:128:16], T.G[:, 2048 * b:2048 * b + 2048:16], T.EK[:, 0:8], False, False, Gk(b) + ["EK"], X)
+        calls = [lambda i=i, k=k: tt(T.VM[:, h + 128 * k:h + 128 * k + 128], T.G[:, 2048 * b + k:2048 * b + 2048:16],
+                                     ps[X][:, 128 * i:128 * i + 128], A.min, Gk(b), [("VM", b % 2, k)], [X])
+                 for i, k in enumerate(CH[c])]
+        if later:
+            return calls
+        for f in calls:
+            f()
 
     def sums(b, c):
         X, h = 5 + b % 2, 2048 * (b % 2)
+        if c == 0:
+            mm(ps[X][:, 0:128:16], T.G[:, 2048 * b:2048 * b + 2048:16], T.EK[:, 0:8], True, True, Gk(b) + ["EK"], X)
         for k in CH[c]:
-            mm(ps[X][:, k:128:16], T.VM[:, h + 128 * k:h + 128 * k + 128], ones, False, k == 15, [("VM", b % 2, k), "EK"], X)
+            mm(ps[X][:, k:128:16], T.VM[:, h + 128 * k:h + 128 * k + 128], ones, True, True, [("VM", b % 2, k), "EK"], X)
+
+    def square(b):
+        i = b % 2
+        E("s", lambda e: e.activation(T["SQ%d" % i][:, 1:129], T.wT[:, 128 * i:128 * i + 128], F.Square, bias=120.0, scale=16.0),
+          [("wT", i)], [("SQ", i)])
 
     def vcopy(b):
         X = 5 + b % 2
-        cp(T["Vt%d" % (b % 2)][:, 1:129], ps[X][:, 0:128], (), [("Vt", b % 2)], [X])
+        tt(T["Vt%d" % (b % 2)][:, 1:129], ps[X][:, 0:128], T["SQ%d" % (b % 2)][:, 0:128], A.add, [("SQ", b % 2)], [("Vt", b % 2)], [X])
 
     def turn(b):
         X, V, K = 5 + b % 2, T["Vt%d" % (b % 2)], [("Vt", b % 2)]
+        mm(ps[X][:, 128:256], V[:, 1:129], T.ID[:], True, True, K + ["ID"], X)
         if b == 3:
             mm(ps[X][:, 256:384], V[:, 1:129], T.ID[:], True, False, K + ["ID"], X)
             mm(ps[X][:, 256:384], V[:, 0:128], T.NID[:], False, True, K + ["NID"], X)
-        mm(ps[X][:, 128:256], V[:, 1:129], T.ID[:], True, True, K + ["ID"], X)
 
     def vs(b):
         X, j = 5 + b % 2, 128 * b
@@ -312,15 +305,12 @@ def rank_program(g, core, T, topo):
 
     def cracks(b):
         X, j = 5 + b % 2, 128 * b
-        ts(T.CC[:, j:j + 128], ps[X][:, 256:384], c1(THR), None, A.is_gt, None, [("col", THR)], [("CC", b)], [X])
-        ts(T.CC[:, 512 + j:640 + j], ps[X][:, 256:384], c1(NTHR), None, A.is_lt, None, [("col", NTHR)], [("CD", b)], [X])
-
-    def crack(b):
-        j = 128 * b
-        tt(T.cr[:, j:j + 128], T.CC[:, j:j + 128], T.CC[:, 512 + j:640 + j], A.add, [("CC", b), ("CD", b)], [("cr", b)])
+        return [lambda: ts(T.nd[:], ps[X][:, 256:384], -1.0, None, A.mult, None, (), ["nd"], [X]),
+                lambda: tt(T.ad[:], ps[X][:, 256:384], T.nd[:], A.max, ["nd"], ["ad"], [X]),
+                lambda: ts(T.CC[:, j:j + 128], T.ad[:], c1(THR), None, A.is_gt, None, ["ad", ("col", THR)], [("CC", b)])]
 
     VSk = [("VS", b) for b in range(4)]
-    CCk = [("CC", b) for b in range(4)] + [("CD", b) for b in range(4)]
+    CCk = [("CC", b) for b in range(4)]
     sent = [0]
 
     def send(t, out, src, R):
@@ -332,142 +322,175 @@ def rank_program(g, core, T, topo):
         sent[0] += len(eg)
         return len(eg)
 
+    def g5(t, a, n):
+        cp(T["cU_%d" % t][:, a:a + n], T.Bt[:, 0:DUMP].indirect(T.nx[:, a // 16:(a + n) // 16]), Bk + BM + ["nx"],
+           [("cU", t, x) for x in range(a // 128, (a + n) // 128)])
+
     for t in range(ROUNDS):
         cU, c16, Dn, pU = T["cU_%d" % t], T["c16_%d" % t], T["Dn_%d" % t], T["pU_%d" % t]
         C16 = [("c16", t)]
-        xg("s", t, 48, 80)
-        xg("v", t, 0, 48)
-        xg("v", t, 128, 32)
-        xg("s", t, 160, 96)
-        xg("s", t, 256, 128)
-        xg("s", t, 384, 128)
-        send(t, T["rC_%d" % t][:], cU[:, 256:512], [("cU", t, x) for x in range(4)])
-        ediag(0)
-        zone1(0)
-        zone2(0)
-        zone3(0)
-        ts(c16[:], cU[:], -2048.0, None, A.add, None, [("cU", t, x) for x in range(4)], C16)
-        for b in range(NB):
-            pen(b, 0)
-            pen(b, 1)
-            sel(b, 0)
-            if b:
-                turn(b - 1)
-                vs(b - 1)
-            sel(b, 1)
-            if b:
-                diff(b - 1)
-            pen(b, 2)
-            if b:
-                cracks(b - 1)
-            sel(b, 2)
-            if b:
-                crack(b - 1)
-            if b < 3:
-                ediag(b + 1)
-                zone1(b + 1)
-            corr(b)
-            sums(b, 0)
-            pen(b, 3)
-            sel(b, 3)
-            sums(b, 1)
-            sums(b, 2)
-            if b < 3:
-                zone2(b + 1)
-                zone3(b + 1)
-            sums(b, 3)
-            vcopy(b)
-            if t == 0 and b < 3:
-                (lambda: unpack(0), lambda: unpack(1), late_constants)[b]()
-        for b in range(NB):
-            bg("s", t, 128 * b, 128)
-        turn(3)
-        cracks(3)
-        vs(3)
-        crack(3)
-        for q in range(16):
-            mm(ps[7][:, 64:128], T.LO[:, 128 * q:128 * q + 128], T.CC[:, q::16], q == 0, q == 15, CCk + [("LO", q)], 7)
-        mm(ps[0][:, 0:256], T.DM[:], T.VS[:, 256:512], True, True, VSk + ["DM"], 0)
-        for q in range(16):
-            mm(ps[3][:, 256:288], T.LW[:, 128 * q:128 * q + 128], T.VS[:, q::16], q == 0, q == 15, VSk + [("LW", q)], 3)
-        E("v", lambda e: e.tensor_reduce(T.Rr[:], ps[7][:, 64:128], AxisListType.X, A.add), (), ["Rr"], [7])
-        cp(T.n2s[:], ps[7][:, 96:128], (), ["n2s"], [7])
-        mm(ps[4][:, 256:257], T.BOf[:], T.Rr[:], True, True, ["BOf", "Rr"], 4)
-        mm(ps[1][:, 0:256], T.DM[:], T.VS[:, 0:256], True, True, VSk + ["DM"], 1)
-        cp(Dn[:, 256:512], ps[0][:, 0:256], (), [("Dn", t, 1)], [0])
-        send(t, T["rD_%d" % t][:], Dn[:, 256:512], [("Dn", t, 1)])
-        tt(T.nn[:], ps[7][:, 64:96], T.n2s[:], A.add, ["n2s"], ["nn"], [7])
-        cts("na", "nn", 5.5, float(DUMP), A.is_gt, A.mult)
-        ctt("rp", "na", "iL", A.add)
-        ts(T.Hs[:], ps[3][:, 256:288], c1(H0), None, A.add, None, [("col", H0)], ["Hs"], [3])
-        Ac = ps[4][:, 256:257]
-        ts(T.i1[:], T.Hs[:], Ac, 512.0, A.add, A.mult, ["Hs"], ["i1"], [4])
-        cts("i2", "i1", 3584, None, A.bitwise_and)
-        ctt("pf", "i2", "rp", A.add)
-        cp(pU[:], T.pf[:], ["pf"], [("pU", t)])
-        ne = 3 * send(t, T["rP_%d" % t][:], pU[:, 16:32], [("pU", t)])
-        mm(ps[6][:], T.ID16[:], c16[:], True, False, C16 + ["ID16"], 6)
-        mm(ps[6][:], T.C16[:], T.ON16[:], False, True, ["C16", "ON16"], 6)
+        last = t == ROUNDS - 1
 
-        def bdiag(b):
-            X = (2, 3)[b % 2]
-            for k in range(1, 16):
+        def bdiag(b, k0=1, k1=16):
+            X = (2, 6)[b % 2]
+            for k in range(k0, k1):
                 mm(ps[X][:, k:128:16], T.GB[:, 2048 * b + k:2048 * b + 2048:16], T.DK[:, 8 * k:8 * k + 8], True, True,
                    keys("GB", 128 * b, 128) + ["DK"], X)
 
+        xg("s", t, 64, 64)
+        xg("v", t, 0, 64)
+        xg("v", t, 128, 32)
+        xg("s", t, 160, 96)
+        ediag(0)
+        Z = zone1(0)
+        Z[0]()
+        if t:
+            g5(t, 256, 256)
+        Z[1]()
+        send(t, T["rC_%d" % t][:], cU[:, 256:512], [("cU", t, x) for x in range(4)])
+        zone2(0)
+        zone3(0)
+        square(0)
+        xg("s", t, 256, 128)
+        ts(c16[:], cU[:], -2048.0, None, A.add, None, [("cU", t, x) for x in range(4)], C16)
+        for b in range(NB):
+            C, Z, nop = [], [], (lambda: 0)
+            pen(b, 0)
+            pen(b, 1)
+            if b:
+                turn(b - 1)
+                C = cracks(b - 1)
+            sel(b, 0)
+            if b:
+                vs(b - 1)
+                diff(b - 1)
+            sel(b, 1)
+            if t == 0 and b < 2:
+                unpack(2 * b)
+            pen(b, 2)
+            if b < 3:
+                ediag(b + 1)
+            pen(b, 3)
+            if b < 3:
+                Z = zone1(b + 1)
+                fg, a = (xg, 384) if b == 0 else (bg, 128 * b - 128 if t else 0)
+            C, Z = C or [nop] * 3, Z or [nop] * 2
+            sums(b, 0)
+            S = sel(b, 2, True) + sel(b, 3, True)
+            for f in (C[0], S[0], C[1], S[1], C[2], S[2], Z[0], S[3], Z[1], S[4]):
+                f()
+            if b < 3:
+                if t or b != 1:
+                    fg("s", t, a, 64)
+                square(b + 1)
+                if t or b != 1:
+                    fg("s", t, a + 64, 64)
+                zone2(b + 1)
+            sums(b, 1)
+            for f in S[5:]:
+                f()
+            if b < 3:
+                zone3(b + 1)
+            if t == 0 and b < 2:
+                unpack(2 * b + 1)
+            sums(b, 2)
+            sums(b, 3)
+            vcopy(b)
+        for b in (2,) if t else (1, 2):
+            bg("s", t, 128 * b, 128)
+        bg("s", t, 384, 64)
+        mm(ps[1][:, 0:256], T.DM[:], T.VS[:, 0:256], True, True, VSk[:2] + ["DM"], 1)
+        turn(3)
+        bdiag(0, 1, 6)
+        vs(3)
+        C = cracks(3)
+        C[0]()
+        cp(Dn[:, 0:256], ps[1][:, 0:256], (), [("Dn", t, 0)], [1])
+        C[1]()
+        mm(ps[0][:, 0:256], T.DM[:], T.VS[:, 256:512], True, True, VSk[2:] + ["DM"], 0)
+        cp(Dn[:, 256:512], ps[0][:, 0:256], (), [("Dn", t, 1)], [0])
+        C[2]()
+        for q in range(16):
+            mm(ps[3][:, 256:288], T.LW[:, 128 * q:128 * q + 128], T.VS[:, q::16], q == 0, q == 15, VSk + [("LW", q)], 3)
+        for q in range(16):
+            mm(ps[4][:, 256:288], T.LO[:, 128 * q:128 * q + 128], T.CC[:, q::16], q == 0, q == 15, CCk + [("LO", q)], 4)
+        bg("v", t, 480, 32)
+        ts(T.Hs[:], ps[3][:, 256:288], c1(H0), None, A.add, None, [("col", H0)], ["Hs"], [3])
+        E("v", lambda e: e.tensor_reduce(T.Rr[:], ps[4][:, 256:288], AxisListType.X, A.add), (), ["Rr"], [4])
+        mm(ps[3][:, 320:321], T.BOf[:], T.Rr[:], True, True, ["BOf", "Rr"], 3)
+        send(t, T["rD_%d" % t][:], Dn[:, 256:512], [("Dn", t, 1)])
+        ts(T.na[:], ps[4][:, 256:288], 5.5, float(DUMP), A.is_gt, A.mult, (), ["na"], [4])
+        ts(T.na1[:], ps[4][:, 256:288], 5.5, None, A.is_gt, None, (), ["na1"], [4])
+        ctt("rp", "na", "iL", A.add)
+        ctt("y1", "na1", "mL", A.mult)
+        Ac = ps[3][:, 320:321]
+        ts(T.i1[:], T.Hs[:], Ac, 512.0, A.add, A.mult, ["Hs"], ["i1"], [3])
+        ts(T.x1[:], T.Hs[:], 37.0, Ac, A.mult, A.add, ["Hs"], ["x1"], [3])
+        cts("i2", "i1", 3584, None, A.bitwise_and)
+        cts("x2", "x1", 4095, None, A.bitwise_and)
+        ctt("pf", "i2", "rp", A.add)
+        ctt("y3", "x2", "y1", A.max)
+        cp(pU[:], T.pf[:], ["pf"], [("pU", t)])
+        cp(T.nx[:], T.y3[:], ["y3"], ["nx"])
+        ne = 3 * send(t, T["rP_%d" % t][:], pU[:, 16:32], [("pU", t)])
+
         def bturn(b):
             s = slice(128 * b, 128 * b + 128)
-            act(T.BT[:, s], ps[(2, 3)[b % 2]][:, 0:128], (), [("BT", b)], [(2, 3)[b % 2]])
-            mm(ps[5][:, s], T.BT[:, s], T.ID16[:], True, False, [("BT", b), "ID16"], 5)
-            mm(ps[5][:, s], T.NID16[:], c16[:, s], False, True, C16 + ["NID16"], 5)
+            act(T.BT[:, s], ps[(2, 6)[b % 2]][:, 0:128], (), [("BT", b)], [(2, 6)[b % 2]])
+            X = MB[b]
+            mm(ps[X][:, s], T.BT[:, s], T.ID16[:], True, False, [("BT", b), "ID16"], X)
+            mm(ps[X][:, s], T.NID16[:], c16[:, s], False, True, C16 + ["NID16"], X)
 
-        bdiag(0)
+        def mend(a, z):
+            s = slice(128 * a, 128 * z)
+            tt(T.t2[:, s], ps[MB[a]][:, s], T.CC[:, s], A.mult, [("CC", b) for b in range(a, z)], [("t2", a)], [MB[a]])
+            tt(T.Bt[:, MEND + 128 * a:MEND + 128 * z], T.t2[:, s], ps[7][:, s], A.add, [("t2", a)], [("Bm", a)], [7])
+
+        cp(T.Dt[:].indirect(pU[:, 0:16]), Dn[:, 0:256], [("pU", t), ("Dn", t, 0)], Dk)
+        bg("v", t, 448, 32)
+        bdiag(0, 6, 16)
         for b in range(NB):
             if b < 3:
                 bdiag(b + 1)
             bturn(b)
-        cp(Dn[:, 0:256], ps[1][:, 0:256], (), [("Dn", t, 0)], [1])
-        ts(T.x1[:], T.Hs[:], 37.0, Ac, A.mult, A.add, ["Hs"], ["x1"], [4])
-        cts("x2", "x1", 4095, None, A.bitwise_and)
-        cts("na1", "nn", 5.5, None, A.is_gt)
-        ctt("y1", "mL", "x2", A.subtract)
-        ctt("y2", "y1", "na1", A.mult)
-        ctt("y3", "y2", "x2", A.add)
-        cp(T.nx[:], T.y3[:], ["y3"], ["nx"])
-        cp(T.Dt[:].indirect(pU[:, 0:16]), Dn[:, 0:256], [("pU", t), ("Dn", t, 0)], Dk)
-        cp(T.Bt[:].indirect(pU[:, 0:16]), cU[:, 0:256], [("pU", t), ("cU", t, 0), ("cU", t, 1)], Bk + ["Bm"])
+            if b in (0, 1):
+                act(ps[7][:, 256 * b:256 * b + 256], c16[:, 256 * b:256 * b + 256], C16, (), [7], bias=2048.0)
+        cp(T.Bt[:].indirect(pU[:, 0:16]), cU[:, 0:256], [("pU", t), ("cU", t, 0), ("cU", t, 1)], Bk + BM)
+        mend(0, 2)
         wr[("arr", t)] = ("arr%d" % t, ne)
         rP = T["rP_%d" % t][:]
         win = T.Bt[:, 0:DUMP]
-        B5 = Bk + ["Bm", "nx"]
+        B5 = Bk + BM + ["nx"]
 
         def rscat(w):
             if w:
                 cp(T.Dt[:].indirect(rP), T["rD_%d" % t][:], [("arr", t)], Dk)
             else:
-                cp(T.Bt[:].indirect(rP), T["rC_%d" % t][:], [("arr", t)], Bk + ["Bm"])
+                cp(T.Bt[:].indirect(rP), T["rC_%d" % t][:], [("arr", t)], Bk + BM)
 
-        rscat(t == ROUNDS - 1)
-        rscat(t < ROUNDS - 1)
-        tt(T.t2[:], ps[5][:], T.cr[:], A.mult, [("cr", b) for b in range(4)], ["t2"], [5])
-        tt(T.Bt[:, MEND:MEND + 512], T.t2[:], ps[6][:], A.add, ["t2"], ["Bm"], [6])
-        if t < ROUNDS - 1:
-            nU = T["cU_%d" % (t + 1)]
-            cp(nU[:, 0:128], win.indirect(T.nx[:, 0:8]), B5, [("cU", t + 1, 0)])
-            cp(nU[:, 128:512], win.indirect(T.nx[:, 8:32]), B5, [("cU", t + 1, x) for x in (1, 2, 3)])
+        rscat(last)
+        if last:
+            rscat(False)
+        mend(2, 4)
+        if not last:
+            rscat(True)
+            g5(t + 1, 0, 128)
+            g5(t + 1, 128, 128)
         else:
             for h in (0, 1):
                 cp(T.ycs[:, h::2], win.indirect(T.nx[:, 16 * h:16 * h + 16]), B5, [("yc", h)])
 
     for i in range(8):
         sl = slice(512 * i, 512 * i + 512)
-        mm(ps[i][:], T.SX[:], T.Dt[:, sl], True, True, Dk + ["SX"], i)
+        X = (1, 2, 3, 4, 6, 1, 2, 3)[i]
+        mm(ps[X][:], T.SX[:], T.Dt[:, sl], True, True, Dk + ["SX"], X)
+        if i < 6:
+            E("s", lambda e: e.activation(T.xin[:, sl], ps[X][:], F.Copy, bias=127.5), (), [("xo", i)], [X])
+        else:
+            ts(T.xin[:, sl], ps[X][:], 127.5, None, A.add, None, (), [("xo", i)], [X])
         if i % 2:
-            E("s", lambda e: e.activation(T.xin[:, sl], ps[i][:], F.Copy, bias=127.5), (), [("xo", i)], [i])
             c = slice(512 * (i - 1), 512 * (i + 1))
             DMA("y", T.yx[:, c], T.xin[:, c], "o%d" % (i // 2), [("xo", i - 1), ("xo", i)])
-        else:
-            ts(T.xin[:, sl], ps[i][:], 127.5, None, A.add, None, (), [("xo", i)], [i])
     DMA("s", T.yc[:], T.ycs[:], "o4", [("yc", 0), ("yc", 1)])
     waits("g", [(s_, 16) for s_ in SEMAPHORES if s_[0] == "o" or (s_[0] == "l" and s_ != "loc")])
     waits("g", [("loc", sent[0])] + [(qsem[q], cnt[q]) for q in qsem])

from concourse.mybir import dt, AluOpType, AxisListType, ActivationFunctionType

A = AluOpType
F = ActivationFunctionType
ROUNDS = 4
NB = 4
W = 4096
MEND = 4096
DUMP = 4608
WIN = DUMP + 4096
LONG = {"f": "float32", "b": "bfloat16", "h": "float16", "i": "int32", "u": "uint16"}
SCRATCH = {}
_spec = """Dt:8704b Bt:8704i xin:4096b pin:2048i ci:512i wi:1i G:8192b GB:8192h VM:4096b R1:256f wT:256b Wz:256b SQ0:136f SQ1:136f
Vt0:144b Vt1:144b VS:512b CC:512b nd:128b ad:128b BT:512h t2:512f ycs:512f Rr:1f Hs:32f na:32f na1:32f rp:32f
i1:32i i2:32i pf:32f x1:32i x2:32i y1:32f y3:32f nx:32u pc:1i ki:1i gi:1i si:1i col:32f wb:1b J:128i Jk:128i Js:128i
Jg:128i K8:128i S8:128i G8:128i K16:16i iL:32f mL:32f iL0:32i mL0:32i u1:128f u2:128f v1:128f v2:128f colk:16f
BO:128b BW:128b BOf:128f BS:128b ID:128b NID:128b ID16:128h NID16:128h EK:128b DK:128h DM:128b DC:128b SX:128b
PL:2048b LO:2048b LW:2048b"""
for _t in range(ROUNDS):
    _spec += " cU_%d:512u c16_%d:512h Dn_%d:512b pU_%d:32u rC_%d:256u rD_%d:256b rP_%d:16u" % ((_t,) * 7)
for _w in _spec.split():
    _n, _d = _w.split(":")
    SCRATCH[_n] = ("sbuf", [128, int(_d[:-1])], LONG[_d[-1]])
for _t in range(8):
    SCRATCH["ps%d" % _t] = ("psum", [128, 512], "float32")
SEMAPHORES = "qv qs qt qg loc lci lwt lx0 lx1 lx2 lx3 lp0 lp1 arr0 arr1 arr2 arr3 o0 o1 o2 o3 o4".split()
K_, G_, S_, P_, P1, G16, G32, IS15, WSC, THR, DBI, H0, WF, K1 = range(14)


def rank_program(g, core, T, topo):
    rank = T.rank_of(core)
    if rank is None:
        return
    eng = {"v": g.vector, "s": g.scalar, "t": g.tensor, "g": g, "y": g.sync}
    qsem = {"v": "qv", "s": "qs", "t": "qt", "g": "qg"}
    cnt = {q: 0 for q in eng}
    know = {q: {} for q in eng}
    snap, wr, rd, bank = {}, {}, {}, {}

    def waits(q, deps):
        best = {}
        for s_, n_ in deps:
            best[s_] = max(best.get(s_, 0), n_)
        for s_ in sorted(best, key=lambda z: -best[z]):
            n_ = best[s_]
            if know[q].get(s_, 0) >= n_:
                continue
            eng[q].wait_ge(T.sem[s_], n_)
            for k2, v2 in list(snap.get((s_, n_), {}).items()) + [(s_, n_)]:
                know[q][k2] = max(know[q].get(k2, 0), v2)

    def prep(q, R, Wk, X):
        deps = [wr[k] for k in list(R) + list(Wk) if k in wr]
        for k in Wk:
            deps += list(rd.get(k, {}).items())
        for k in X:
            deps += [d for d in bank.get(k, {}).items() if d[0] != qsem.get(q)]
        waits(q, deps)

    def mark(tok, q, R, Wk, X):
        d = dict(know[q])
        d[tok[0]] = tok[1]
        snap[tok] = d
        for k in R:
            rd.setdefault(k, {})[tok[0]] = tok[1]
        for k in Wk:
            wr[k] = tok
            rd[k] = {}
        for k in X:
            bank.setdefault(k, {})[tok[0]] = tok[1]

    def E(q, call, R=(), Wk=(), X=()):
        prep(q, R, Wk, X)
        cnt[q] += 1
        call(eng[q]).then_inc(T.sem[qsem[q]], 1)
        mark((qsem[q], cnt[q]), q, R, Wk, X)

    def DMA(q, out, in_, sem, R=(), Wk=()):
        prep(q, R, Wk, ())
        eng[q].dma_start(out, in_).then_inc(T.sem[sem], 16)
        mark((sem, 16), q, R, Wk, ())

    ps = [T["ps%d" % i] for i in range(8)]

    def c1(i):
        return T.col[:, i:i + 1]

    def mm(out, l, r, a, b, R, X):
        E("t", lambda e: e.matmul(out, l, r, a, b), R, (), [X])

    def ts(out, i, s1, s2, o1, o2=None, R=(), Wk=(), X=()):
        if o2 is None:
            E("v", lambda e: e.tensor_scalar(out, i, s1, None, o1), R, Wk, X)
        else:
            E("v", lambda e: e.tensor_scalar(out, i, s1, s2, o1, o2), R, Wk, X)

    def tt(out, a, b, op, R=(), Wk=(), X=()):
        E("v", lambda e: e.tensor_tensor(out, a, b, op), R, Wk, X)

    def cp(out, i, R=(), Wk=(), X=()):
        E("v", lambda e: e.tensor_copy(out, i), R, Wk, X)

    def act(out, i, R=(), Wk=(), X=(), bias=0.0, scale=1.0):
        E("s", lambda e: e.activation(out, i, F.Identity, bias=bias, scale=scale), R, Wk, X)

    def cts(o, i, s1, s2, o1, o2=None, cols=()):
        ts(T[o][:], T[i][:], s1, s2, o1, o2, [i] + [("col", c) for c in cols or ()], [o])

    def ctt(o, a, b, op):
        tt(T[o][:], T[a][:], T[b][:], op, [a, b], [o])

    def colv(i, src, s1, s2, o1, o2=None):
        ts(c1(i), T[src][:], s1, s2, o1, o2, [src], [("col", i)])

    DMA("y", T.ci[:], T.cb[:], "lci", Wk=["ci"])
    DMA("s", T.wi[:], T.wt[:], "lwt", Wk=["wi"])
    for i in range(4):
        DMA("ys"[i % 2], T.xin[:, 1024 * i:1024 * i + 1024], T.x[:, 1024 * i:1024 * i + 1024], "lx%d" % i, Wk=[("xin", i)])
    for i in range(2):
        DMA("ys"[i % 2], T.pin[:, 1024 * i:1024 * i + 1024], T.pk[:, 1024 * i:1024 * i + 1024], "lp%d" % i, Wk=[("pin", i)])

    for buf, pat, base, cm in (("pc", [[0, 1]], 0, 1), ("J", [[1, 128]], 0, 0), ("K8", [[1, 16], [0, 8]], 0, 0),
                               ("G8", [[0, 16], [1, 8]], 0, 0), ("K16", [[1, 16]], 0, 0),
                               ("iL0", [[1, 2], [32, 16]], 0, 2), ("mL0", [[16, 32]], MEND, 1)):
        E("g", lambda e: e.iota(T[buf][:], pat, base, cm), (), [buf])
    for i in (0, 1):
        E("v", lambda e: e.memset(ps[3 + i][:, 0:128], -7.5), (), (), [3 + i])
        E("v", lambda e: e.memset(T["Vt%d" % i][:, 0:16], 0.0), (), [("Vt", i)])
        E("v", lambda e: e.memset(T["SQ%d" % i][:, 0:8], 0.0), (), [("SQ", i)])
    cts("ki", "pc", 15, None, A.bitwise_and)
    cts("gi", "pc", 4, None, A.arith_shift_right)
    cts("Jk", "J", 15, None, A.bitwise_and)
    cts("Jg", "J", 4, None, A.arith_shift_right)
    colv(P_, "pc", 0.0, None, A.add)
    colv(P1, "pc", 1.0, None, A.add)
    colv(G_, "gi", 0.0, None, A.add)
    cts("u1", "Jk", 15.0, -16.0, A.is_equal, A.mult)
    cts("u2", "Jk", 7.0, 1000.0, A.is_equal, A.mult)
    colv(DBI, "ki", 7.0, -127.5, A.is_equal, A.mult)
    cts("ID", "J", c1(P_), None, A.is_equal, None, [P_])
    ctt("u1", "u1", "u2", A.add)
    cts("BO", "Jg", c1(G_), None, A.is_equal, None, [G_])
    cts("si", "ki", 8.0, None, A.add)
    cts("S8", "K8", 8.0, None, A.add)
    ctt("u1", "u1", "J", A.add)
    cts("Js", "J", 8.0, None, A.add)
    cts("si", "si", 15, None, A.bitwise_and)
    cts("S8", "S8", 15, None, A.bitwise_and)
    cts("u2", "u1", 1.0, c1(P_), A.add, A.is_equal, [P_])
    cts("Js", "Js", 15, None, A.bitwise_and)
    colv(S_, "si", 0.0, None, A.add)
    ctt("DM", "ID", "u2", A.subtract)
    cts("v1", "G8", c1(G_), None, A.is_equal, None, [G_])
    cts("v2", "S8", c1(S_), None, A.is_le, None, [S_])
    cts("wb", "wi", 0.0, None, A.add)
    colv(WF, "wi", 0.0, None, A.add)
    ctt("EK", "v1", "v2", A.mult)
    act(T.ID16[:], T.ID[:], ["ID"], ["ID16"])
    act(T.NID[:], T.ID[:], ["ID"], ["NID"], scale=-1.0)
    act(T.NID16[:], T.ID[:], ["ID"], ["NID16"], scale=-1.0)
    act(T.BOf[:], T.BO[:], ["BO"], ["BOf"])
    cts("BW", "BO", c1(WF), None, A.mult, None, [WF])
    for o, i in (("LO", "BO"), ("LW", "BW")):
        for q in range(16):
            E("g", lambda e: e.affine_select(T[o][:, 128 * q:128 * q + 128], T[i][:], [[0, 8], [1, 16]], A.is_equal, 0.0, -q, 0),
              [i], [(o, q)])
    colv(K_, "ki", 0.0, None, A.add)
    colv(K1, "ki", 1.0, None, A.add)
    colv(IS15, "ki", 15.0, None, A.is_equal)
    colv(WSC, "ki", 15.0, None, A.not_equal)
    cts("u1", "Js", -7.0, 512.0, A.add, A.mult)
    cts("colk", "K16", c1(K1), -512.0, A.is_equal, A.mult, [K1])
    cts("u2", "J", c1(P1), None, A.is_equal, None, [P1])
    cts("u1", "u1", c1(IS15), c1(WSC), A.mult, A.add, [IS15, WSC])
    cts("colk", "colk", c1(IS15), None, A.add, None, [IS15])
    ctt("u2", "u2", "BO", A.mult)
    ctt("BS", "u1", "BO", A.mult)
    colv(THR, "ki", 0.0, 1.0e6, A.is_equal, A.mult)
    ctt("DC", "ID", "u2", A.subtract)
    for k in range(1, 16):
        ts(T.PL[:, 128 * k:128 * k + 128], T.BS[:], T.colk[:, k:k + 1], None, A.mult, None, ["BS", "colk"], [("PL", k)])
    ts(c1(THR), c1(THR), 96.25, None, A.add, None, [("col", THR)], [("col", THR)])
    for h in (0, 1):
        cp(T.cU_0[:, 256 * h:256 * h + 256], T.ci[:, h::2], ["ci"], [("cU", 0, 2 * h), ("cU", 0, 2 * h + 1)])
    mm(ps[4][:, 300:301], T.BO[:], T.wb[:], True, True, ["BO", "wb"], 4)
    colv(G32, "gi", 32.0, None, A.mult)
    colv(G16, "gi", 16.0, None, A.mult)
    cts("u1", "K8", c1(K_), None, A.is_equal, None, [K_])
    cts("u2", "Js", c1(S_), None, A.is_le, None, [S_])
    cts("iL", "iL0", c1(G32), None, A.subtract, None, [G32])
    cts("mL", "mL0", c1(G16), None, A.subtract, None, [G16])
    ctt("DK", "u1", "v1", A.mult)
    ctt("SX", "u2", "BO", A.mult)
    ts(c1(H0), ps[4][:, 300:301], 127.5, None, A.mult, None, (), [("col", H0)], [4])

    for i in range(8):
        sl, X = slice(512 * i, 512 * i + 512), (0, 1, 2, 5, 6, 7)[i % 6]
        mm(ps[X][:], T.DM[:], T.xin[:, sl], True, True, ["DM", ("xin", i // 2)], X)
        if i in (3, 7):
            ts(T.Dt[:, sl], ps[X][:], c1(DBI), None, A.add, None, [("col", DBI)], [("Dt", i)], [X])
        else:
            act(T.Dt[:, sl], ps[X][:], [("col", DBI)], [("Dt", i)], [X], bias=c1(DBI))
    Dk = [("Dt", i) for i in range(8)]
    Bk = [("Bt", i) for i in range(8)]

    def unpack(i):
        s, n = i // 2, 1024 * (i // 2) + 512 * (i % 2)
        j = T.pin[:, n:n + 512]
        ts(T.Bt[:, n:n + 512], j, 4095, None, A.bitwise_and, None, [("pin", s)], [("Bt", i)])
        ts(T.Bt[:, 2048 + n:2560 + n], j, 12, None, A.arith_shift_right, None, [("pin", s)], [("Bt", 4 + i)])

    BM, MB = [("Bm", 0), ("Bm", 2)], (5, 5, 0, 0)
    ones = T.EK[:, 64:72]

    def keys(n, a, m):
        return [(n, x) for x in range(a // 16, (a + m) // 16)]

    def gath(q, dst, win, t, a, n, R, Wk, bias=0.0):
        w = win.indirect(T["cU_%d" % t][:, a:a + n])
        out = dst[:, 16 * a:16 * (a + n)]
        R = R + [("cU", t, x) for x in range(a // 128, (a + n + 127) // 128)]
        if q == "s":
            act(out, w, R, Wk, bias=bias)
        elif bias:
            ts(out, w, bias, None, A.add, None, R, Wk)
        else:
            cp(out, w, R, Wk)

    def xg(q, t, a, n):
        gath(q, T.G, T.Dt[:, 0:W], t, a, n, Dk, keys("G", a, n))

    def bg(q, t, a, n):
        gath(q, T.GB, T.Bt[:, 0:W], t, a, n, Bk, keys("GB", a, n), -2048.0)

    def Gk(b):
        return keys("G", 128 * b, 128)

    def ediag(b):
        X = 3 + b % 2
        for k in range(15):
            mm(ps[X][:, k:128:16], T.G[:, 2048 * b + k:2048 * b + 2048:16], T.EK[:, 8 * k:8 * k + 8], True, True, Gk(b) + ["EK"], X)

    def zone1(b):
        X, h, i = 3 + b % 2, 128 * (b % 2), b % 2
        C = 1.5 * 2.0 ** 27
        return [lambda: ts(T.R1[:, h:h + 128], ps[X][:, 0:128], C, C, A.add, A.subtract, (), [("R1", i)], [X]),
                lambda: tt(T.wT[:, h:h + 128], ps[X][:, 0:128], T.R1[:, h:h + 128], A.subtract, [("R1", i)], [("wT", i)], [X])]

    def zone2(b):
        X, h, i = 3 + b % 2, 128 * (b % 2), b % 2
        mm(ps[X][:, 128:256], T.wT[:, h:h + 128], T.ID[:], True, True, [("wT", i), "ID"], X)

    def zone3(b):
        X, h, i = 3 + b % 2, 128 * (b % 2), b % 2
        ts(T.Wz[:, h:h + 128], ps[X][:, 128:256], c1(WSC), c1(IS15), A.mult, A.add, [("col", WSC), ("col", IS15)], [("Wz", i)], [X])

    CH = ((1, 2, 3, 4), (5, 6, 7, 8), (9, 10, 11, 12), (13, 14, 15))

    def pen(b, c):
        X, h = (4 * b + c) % 3, 128 * (b % 2)
        for i, k in enumerate(CH[c]):
            mm(ps[X][:, 128 * i:128 * i + 128], T.PL[:, 128 * k:128 * k + 128], T.Wz[:, h:h + 128], True, True,
               [("PL", k), ("Wz", b % 2)], X)

    def sel(b, c, later=False):
        X, h = (4 * b + c) % 3, 2048 * (b % 2)
        calls = [lambda i=i, k=k: tt(T.VM[:, h + 128 * k:h + 128 * k + 128], T.G[:, 2048 * b + k:2048 * b + 2048:16],
                                     ps[X][:, 128 * i:128 * i + 128], A.min, Gk(b), [("VM", b % 2, k)], [X])
                 for i, k in enumerate(CH[c])]
        if later:
            return calls
        for f in calls:
            f()

    def sums(b, c):
        X, h = 5 + b % 2, 2048 * (b % 2)
        if c == 0:
            mm(ps[X][:, 0:128:16], T.G[:, 2048 * b:2048 * b + 2048:16], T.EK[:, 0:8], True, True, Gk(b) + ["EK"], X)
        for k in CH[c]:
            mm(ps[X][:, k:128:16], T.VM[:, h + 128 * k:h + 128 * k + 128], ones, True, True, [("VM", b % 2, k), "EK"], X)

    def square(b):
        i = b % 2
        E("s", lambda e: e.activation(T["SQ%d" % i][:, 1:129], T.wT[:, 128 * i:128 * i + 128], F.Square, bias=120.0, scale=16.0),
          [("wT", i)], [("SQ", i)])

    def vcopy(b):
        X = 5 + b % 2
        tt(T["Vt%d" % (b % 2)][:, 1:129], ps[X][:, 0:128], T["SQ%d" % (b % 2)][:, 0:128], A.add, [("SQ", b % 2)], [("Vt", b % 2)], [X])

    def turn(b):
        X, V, K = 5 + b % 2, T["Vt%d" % (b % 2)], [("Vt", b % 2)]
        mm(ps[X][:, 128:256], V[:, 1:129], T.ID[:], True, True, K + ["ID"], X)
        if b == 3:
            mm(ps[X][:, 256:384], V[:, 1:129], T.ID[:], True, False, K + ["ID"], X)
            mm(ps[X][:, 256:384], V[:, 0:128], T.NID[:], False, True, K + ["NID"], X)

    def vs(b):
        X, j = 5 + b % 2, 128 * b
        cp(T.VS[:, j:j + 128], ps[X][:, 128:256], (), [("VS", b)], [X])

    def diff(b):
        X, j = 5 + b % 2, 128 * b
        mm(ps[X][:, 256:384], T.DC[:], T.VS[:, j:j + 128], True, True, [("VS", b), "DC"], X)

    def cracks(b):
        X, j = 5 + b % 2, 128 * b
        return [lambda: ts(T.nd[:], ps[X][:, 256:384], -1.0, None, A.mult, None, (), ["nd"], [X]),
                lambda: tt(T.ad[:], ps[X][:, 256:384], T.nd[:], A.max, ["nd"], ["ad"], [X]),
                lambda: ts(T.CC[:, j:j + 128], T.ad[:], c1(THR), None, A.is_gt, None, ["ad", ("col", THR)], [("CC", b)])]

    VSk = [("VS", b) for b in range(4)]
    CCk = [("CC", b) for b in range(4)]
    sent = [0]

    def send(t, out, src, R):
        to = T.cores[(rank + 1 + t % 3) % len(T.cores)]
        eg = topo.engines(core, to)[:8]
        rid, pid, _ = topo.addr(to)
        waits("g", [wr[k] for k in R])
        g.remote_dma(out, src, T.sem["arr%d" % t], T.sem.loc, pid, rid, sum(1 << x for x in eg))
        sent[0] += len(eg)
        return len(eg)

    def g5(t, a, n):
        cp(T["cU_%d" % t][:, a:a + n], T.Bt[:, 0:DUMP].indirect(T.nx[:, a // 16:(a + n) // 16]), Bk + BM + ["nx"],
           [("cU", t, x) for x in range(a // 128, (a + n) // 128)])

    for t in range(ROUNDS):
        cU, c16, Dn, pU = T["cU_%d" % t], T["c16_%d" % t], T["Dn_%d" % t], T["pU_%d" % t]
        C16 = [("c16", t)]
        last = t == ROUNDS - 1

        def bdiag(b, k0=1, k1=16):
            X = (2, 6)[b % 2]
            for k in range(k0, k1):
                mm(ps[X][:, k:128:16], T.GB[:, 2048 * b + k:2048 * b + 2048:16], T.DK[:, 8 * k:8 * k + 8], True, True,
                   keys("GB", 128 * b, 128) + ["DK"], X)

        xg("s", t, 64, 64)
        xg("v", t, 0, 64)
        xg("v", t, 128, 32)
        xg("s", t, 160, 96)
        ediag(0)
        Z = zone1(0)
        Z[0]()
        if t:
            g5(t, 256, 256)
        Z[1]()
        send(t, T["rC_%d" % t][:], cU[:, 256:512], [("cU", t, x) for x in range(4)])
        zone2(0)
        zone3(0)
        square(0)
        xg("s", t, 256, 128)
        ts(c16[:], cU[:], -2048.0, None, A.add, None, [("cU", t, x) for x in range(4)], C16)
        for b in range(NB):
            C, Z, nop = [], [], (lambda: 0)
            pen(b, 0)
            pen(b, 1)
            if b:
                turn(b - 1)
                C = cracks(b - 1)
            sel(b, 0)
            if b:
                vs(b - 1)
                diff(b - 1)
            sel(b, 1)
            if t == 0 and b < 2:
                unpack(2 * b)
            pen(b, 2)
            if b < 3:
                ediag(b + 1)
            pen(b, 3)
            if b < 3:
                Z = zone1(b + 1)
                fg, a = (xg, 384) if b == 0 else (bg, 128 * b - 128 if t else 0)
            C, Z = C or [nop] * 3, Z or [nop] * 2
            sums(b, 0)
            S = sel(b, 2, True) + sel(b, 3, True)
            for f in (C[0], S[0], C[1], S[1], C[2], S[2], Z[0], S[3], Z[1], S[4]):
                f()
            if b < 3:
                if t or b != 1:
                    fg("s", t, a, 64)
                square(b + 1)
                if t or b != 1:
                    fg("s", t, a + 64, 64)
                zone2(b + 1)
            sums(b, 1)
            for f in S[5:]:
                f()
            if b < 3:
                zone3(b + 1)
            if t == 0 and b < 2:
                unpack(2 * b + 1)
            sums(b, 2)
            sums(b, 3)
            vcopy(b)
        for b in (2,) if t else (1, 2):
            bg("s", t, 128 * b, 128)
        bg("s", t, 384, 64)
        mm(ps[1][:, 0:256], T.DM[:], T.VS[:, 0:256], True, True, VSk[:2] + ["DM"], 1)
        turn(3)
        bdiag(0, 1, 6)
        vs(3)
        C = cracks(3)
        C[0]()
        cp(Dn[:, 0:256], ps[1][:, 0:256], (), [("Dn", t, 0)], [1])
        C[1]()
        mm(ps[0][:, 0:256], T.DM[:], T.VS[:, 256:512], True, True, VSk[2:] + ["DM"], 0)
        cp(Dn[:, 256:512], ps[0][:, 0:256], (), [("Dn", t, 1)], [0])
        C[2]()
        for q in range(16):
            mm(ps[3][:, 256:288], T.LW[:, 128 * q:128 * q + 128], T.VS[:, q::16], q == 0, q == 15, VSk + [("LW", q)], 3)
        for q in range(16):
            mm(ps[4][:, 256:288], T.LO[:, 128 * q:128 * q + 128], T.CC[:, q::16], q == 0, q == 15, CCk + [("LO", q)], 4)
        bg("v", t, 480, 32)
        ts(T.Hs[:], ps[3][:, 256:288], c1(H0), None, A.add, None, [("col", H0)], ["Hs"], [3])
        E("v", lambda e: e.tensor_reduce(T.Rr[:], ps[4][:, 256:288], AxisListType.X, A.add), (), ["Rr"], [4])
        mm(ps[3][:, 320:321], T.BOf[:], T.Rr[:], True, True, ["BOf", "Rr"], 3)
        send(t, T["rD_%d" % t][:], Dn[:, 256:512], [("Dn", t, 1)])
        ts(T.na[:], ps[4][:, 256:288], 5.5, float(DUMP), A.is_gt, A.mult, (), ["na"], [4])
        ts(T.na1[:], ps[4][:, 256:288], 5.5, None, A.is_gt, None, (), ["na1"], [4])
        ctt("rp", "na", "iL", A.add)
        ctt("y1", "na1", "mL", A.mult)
        Ac = ps[3][:, 320:321]
        ts(T.i1[:], T.Hs[:], Ac, 512.0, A.add, A.mult, ["Hs"], ["i1"], [3])
        ts(T.x1[:], T.Hs[:], 37.0, Ac, A.mult, A.add, ["Hs"], ["x1"], [3])
        cts("i2", "i1", 3584, None, A.bitwise_and)
        cts("x2", "x1", 4095, None, A.bitwise_and)
        ctt("pf", "i2", "rp", A.add)
        ctt("y3", "x2", "y1", A.max)
        cp(pU[:], T.pf[:], ["pf"], [("pU", t)])
        cp(T.nx[:], T.y3[:], ["y3"], ["nx"])
        ne = 3 * send(t, T["rP_%d" % t][:], pU[:, 16:32], [("pU", t)])

        def bturn(b):
            s = slice(128 * b, 128 * b + 128)
            act(T.BT[:, s], ps[(2, 6)[b % 2]][:, 0:128], (), [("BT", b)], [(2, 6)[b % 2]])
            X = MB[b]
            mm(ps[X][:, s], T.BT[:, s], T.ID16[:], True, False, [("BT", b), "ID16"], X)
            mm(ps[X][:, s], T.NID16[:], c16[:, s], False, True, C16 + ["NID16"], X)

        def mend(a, z):
            s = slice(128 * a, 128 * z)
            tt(T.t2[:, s], ps[MB[a]][:, s], T.CC[:, s], A.mult, [("CC", b) for b in range(a, z)], [("t2", a)], [MB[a]])
            tt(T.Bt[:, MEND + 128 * a:MEND + 128 * z], T.t2[:, s], ps[7][:, s], A.add, [("t2", a)], [("Bm", a)], [7])

        cp(T.Dt[:].indirect(pU[:, 0:16]), Dn[:, 0:256], [("pU", t), ("Dn", t, 0)], Dk)
        bg("v", t, 448, 32)
        bdiag(0, 6, 16)
        for b in range(NB):
            if b < 3:
                bdiag(b + 1)
            bturn(b)
            if b in (0, 1):
                act(ps[7][:, 256 * b:256 * b + 256], c16[:, 256 * b:256 * b + 256], C16, (), [7], bias=2048.0)
        cp(T.Bt[:].indirect(pU[:, 0:16]), cU[:, 0:256], [("pU", t), ("cU", t, 0), ("cU", t, 1)], Bk + BM)
        mend(0, 2)
        wr[("arr", t)] = ("arr%d" % t, ne)
        rP = T["rP_%d" % t][:]
        win = T.Bt[:, 0:DUMP]
        B5 = Bk + BM + ["nx"]

        def rscat(w):
            if w:
                cp(T.Dt[:].indirect(rP), T["rD_%d" % t][:], [("arr", t)], Dk)
            else:
                cp(T.Bt[:].indirect(rP), T["rC_%d" % t][:], [("arr", t)], Bk + BM)

        rscat(last)
        if last:
            rscat(False)
        mend(2, 4)
        if not last:
            rscat(True)
            g5(t + 1, 0, 128)
            g5(t + 1, 128, 128)
        else:
            for h in (0, 1):
                cp(T.ycs[:, h::2], win.indirect(T.nx[:, 16 * h:16 * h + 16]), B5, [("yc", h)])

    for i in range(8):
        sl = slice(512 * i, 512 * i + 512)
        X = (1, 2, 3, 4, 6, 1, 2, 3)[i]
        mm(ps[X][:], T.SX[:], T.Dt[:, sl], True, True, Dk + ["SX"], X)
        if i < 6:
            E("s", lambda e: e.activation(T.xin[:, sl], ps[X][:], F.Copy, bias=127.5), (), [("xo", i)], [X])
        else:
            ts(T.xin[:, sl], ps[X][:], 127.5, None, A.add, None, (), [("xo", i)], [X])
        if i % 2:
            c = slice(512 * (i - 1), 512 * (i + 1))
            DMA("y", T.yx[:, c], T.xin[:, c], "o%d" % (i // 2), [("xo", i - 1), ("xo", i)])
    DMA("s", T.yc[:], T.ycs[:], "o4", [("yc", 0), ("yc", 1)])
    waits("g", [(s_, 16) for s_ in SEMAPHORES if s_[0] == "o" or (s_[0] == "l" and s_ != "loc")])
    waits("g", [("loc", sent[0])] + [(qsem[q], cnt[q]) for q in qsem])
